import numpy as np
import ml_dtypes


def mxq(x, axis, fmt="e4m3"):
    dtype, down = {"e4m3": (ml_dtypes.float8_e4m3fn, 7), "e5m2": (ml_dtypes.float8_e5m2, 14)}[fmt]
    v = np.moveaxis(np.asarray(x, np.float32).astype(ml_dtypes.bfloat16).astype(np.float64), axis, -1)
    blocks = v.reshape(v.shape[:-1] + (-1, 32))
    amax = np.abs(blocks).max(-1, keepdims=True)
    byte = np.maximum(np.where(amax > 0, np.frexp(amax)[1] - 1 + 127, 0) - down, 1)
    scale = np.exp2(byte - 127.0)
    codes = (blocks / scale).astype(np.float32).astype(dtype).astype(np.float64)
    return np.moveaxis((codes * scale).reshape(v.shape), -1, axis)


WIDE = False


def mx_kscale(k):
    if not WIDE:
        return np.ones(k)
    levels = np.array([10, -10, 5, -5, 0])
    if k % 512:
        return np.exp2(np.random.permutation(np.resize(levels, k // 32))).repeat(32)
    a = np.empty((k // 512, 16))
    for p in range(k // 512):
        a[p, :8] = np.random.permutation(np.resize(levels, 8))
        for g in range(8):
            far = levels[np.abs(levels - a[p, g]) >= 10]
            a[p, g + 8] = far[np.random.randint(len(far))]
    return np.exp2(a.ravel()).repeat(32)


def f64(x):
    return np.asarray(x).astype(np.float64)


def striped(idx):
    return np.tile(idx.reshape(-1, 16).T, (8, 1)).astype(np.uint16)


def unstriped(offs):
    return offs[:16].T.reshape(-1).astype(np.int64)


def striped8(idx):
    return np.concatenate([x.reshape(-1, 16).T for x in idx]).astype(np.uint16)


def runs(offs, k):
    lists = np.stack([offs[16 * r : 16 * r + 16].T.reshape(-1) for r in range(8)]).astype(np.int64)
    return lists[np.arange(k) % 512 // 64]


def pack_weight(w):
    k, n = w.shape
    w = f64(np.asarray(w, np.float32).astype(ml_dtypes.bfloat16)).reshape(k // 32, 32, n)
    amax = np.abs(w).max(1)
    byte = np.clip(np.where(amax > 0, np.frexp(amax)[1] - 1 + 127 - 7, 1), 1, 254)
    scaled = (w * np.exp2(127.0 - byte)[:, None, :]).reshape(k, n).astype(np.float32)
    words = np.ascontiguousarray(scaled.reshape(k // 512, 128, 4, n).transpose(0, 1, 3, 2)).astype(ml_dtypes.float8_e4m3fn).view(np.uint8)
    return words, np.ascontiguousarray(byte.astype(np.uint8).reshape(k // 512, 16, n))


def unpack_weight(words, scales):
    g, p, n, _ = words.shape
    vals = np.ascontiguousarray(words).view(ml_dtypes.float8_e4m3fn).astype(np.float64) * np.repeat(np.exp2(scales.astype(np.float64) - 127.0), 8, axis=1)[..., None]
    return vals.transpose(0, 1, 3, 2).reshape(g * 512, n)


def sigmoid(v):
    return 1.0 / (1.0 + np.exp(-np.maximum(v, -700.0)))


K, T, S, N = 512, 2048, 512, 512


def setup_inputs():
    n = np.random.standard_normal
    s = mx_kscale(K)[:, None]
    packed_xT = pack_weight(n((K, T)) * s)
    return {
        "x_words": packed_xT[0],
        "x_scales": packed_xT[1],
        "w1": (n((K, N)) / np.sqrt(2 * K) / s).astype(np.float32),
        "w2": (n((K, N)) / np.sqrt(2 * K) / s).astype(np.float32),
        "w3": (n((K, N)) / np.sqrt(K) / s).astype(np.float32),
        "offs": striped8(np.random.randint(0, T, (8, S))),
        "own": striped(np.random.permutation(T)[:S]),
    }


def reference(x_words, x_scales, w1, w2, w3, offs, own):
    xq = unpack_weight(x_words, x_scales)[np.arange(K)[:, None], runs(offs, K)]
    x_own = unpack_weight(x_words, x_scales)[:, unstriped(own)]
    s = mxq(f64(w3), 0, "e4m3").T @ xq
    return ((mxq(f64(w1), 0, "e4m3").T @ xq + mxq(f64(w2), 0, "e4m3").T @ x_own)) * sigmoid(s)

@@ -1,0 +1,167 @@
+from contextlib import ExitStack
+
+import concourse.mybir as mybir
+
+K, T, S, N = 512, 2048, 512, 512
+FLOPS = 3 * 2 * K * N * S
+
+F32 = mybir.dt.float32
+BF16 = mybir.dt.bfloat16
+I32 = mybir.dt.int32
+U32 = mybir.dt.uint32
+U16 = mybir.dt.uint16
+U8 = mybir.dt.uint8
+FP8X4 = mybir.dt.float8_e4m3fn_x4
+SIGMOID = mybir.ActivationFunctionType.Sigmoid
+MULT = mybir.AluOpType.mult
+
+P = 128
+PACK = 4
+QUAD = 32
+ROWS = 4
+SHIFT = 14
+SPAN = P - QUAD + ROWS
+
+
+def tile_picked_ngramgate_none_p_kernel(tc, x_words, x_scales, w1, w2, w3, offs, own, out):
+    nc = tc.nc
+    with ExitStack() as ctx:
+        keep = ctx.enter_context(tc.tile_pool(name="keep", bufs=1))
+        psum = ctx.enter_context(tc.psum_pool(name="psum", bufs=1))
+
+        offs_sb = keep.tile([P, S // 16], U16, name="offs_sb")
+        own_sb = keep.tile([P, S // 16], U16, name="own_sb")
+        nc.sync.dma_start(offs_sb[:], offs)
+        nc.sync.dma_start(own_sb[:], own)
+
+        byte_table = keep.tile([P, T], U8, name="byte_table", tag="late", align_bytes=64)
+        nc.sync.dma_start(out=byte_table[:].bitcast(I32), in_=x_scales[0].bitcast(I32).unsqueeze(1).broadcast_to([16, 8, T // 4]))
+        x_plane = keep.tile([P, 2 * S], U8, name="x_plane", align_bytes=64)
+        nc.vector.memset(x_plane[:].bitcast(I32), 0)
+        warm_in = keep.tile([P, 1], F32, name="warm_in")
+        warm_out = keep.tile([P, 1], F32, name="warm_out")
+        nc.vector.memset(warm_in[:], 0.0)
+        nc.scalar.activation(warm_out[:], warm_in[:], SIGMOID)
+
+        word_table = keep.tile([P, T], U32, name="word_table", align_bytes=64)
+        weights = {"w1": w1, "w2": w2, "w3": w3}
+        raw = {}
+
+        def load(name, c0, c1):
+            if name == "x":
+                nc.sync.dma_start(out=word_table[:].bitcast(I32), in_=x_words[0].rearrange("p c r -> p (c r)").bitcast(I32))
+                return
+            t = keep.tile([P, PACK, c1 - c0], F32, name="raw_%s_%d" % (name, c0))
+            nc.sync.dma_start(out=t[:], in_=weights[name][:, c0:c1].rearrange("(p j) n -> p j n", j=PACK))
+            for c in range(c0, c1, P):
+                raw[name, c] = (t, c0)
+
+        for item in [("w3", 0, 256), ("x", 0, 0), ("w3", 256, 512)]:
+            load(*item)
+
+        picked_bytes = keep.tile([P, 2 * S], U8, name="picked_bytes", align_bytes=64)
+        nc.vector.tensor_copy(picked_bytes[:, 0:S], byte_table[:].indirect(offs_sb[:]))
+        nc.vector.tensor_copy(picked_bytes[:, S : 2 * S], byte_table[:].indirect(own_sb[:]))
+        for i in range(ROWS):
+            nc.sync.dma_start(out=x_plane[i:P:QUAD, :].bitcast(I32), in_=picked_bytes[8 * i : P : QUAD, :].bitcast(I32))
+
+        late = [("w1", 0, 256), ("w2", 0, 256), ("w1", 256, 512), ("w2", 256, 384), ("w2", 384, 512)]
+        late_raw = keep.tile([P, PACK * sum(c1 - c0 for name, c0, c1 in late)], F32, name="late_raw", tag="late", align_bytes=64)
+        at = 0
+        for name, c0, c1 in late:
+            t = late_raw[:, at : at + PACK * (c1 - c0)].rearrange("p (j n) -> p j n", j=PACK)
+            nc.sync.dma_start(out=t, in_=weights[name][:, c0:c1].rearrange("(p j) n -> p j n", j=PACK))
+            for c in range(c0, c1, P):
+                raw[name, c] = (t, c0)
+            at = at + PACK * (c1 - c0)
+
+        hashed = keep.tile([P, S], U32, name="hashed", align_bytes=64)
+        mine = keep.tile([P, S], U32, name="mine", align_bytes=64)
+        nc.vector.tensor_copy(hashed[:], word_table[:].indirect(offs_sb[:]))
+        nc.vector.tensor_copy(mine[:], word_table[:].indirect(own_sb[:]))
+        moving = {
+            "w1": (hashed, x_plane[:, 0:S]),
+            "w3": (hashed, x_plane[:, 0:S]),
+            "w2": (mine, x_plane[:, S : 2 * S]),
+        }
+
+        grouped = {}
+        quantised = {}
+        gate_ps = [psum.tile([P, S], F32, name="gate_ps%d" % b) for b in range(N // P)]
+        sum_ps = [psum.tile([P, S], F32, name="sum_ps%d" % b) for b in range(N // P)]
+        gates = [keep.tile([P, S], F32, name="gate%d" % b) for b in range(N // P)]
+
+        def cast(engine, name, c0, c1):
+            t, base = raw[name, c0]
+            g = keep.tile([P, c1 - c0, PACK], BF16, name="grouped_%s_%d" % (name, c0), align_bytes=64)
+            dst = g[:].rearrange("p (c i) t -> p c t i", i=4)
+            src = t[:, :, c0 - base : c1 - base].rearrange("p t (c i) -> p c t i", i=4)
+            if engine == "s":
+                nc.scalar.copy(dst, src)
+            else:
+                nc.vector.tensor_copy(dst, src)
+            grouped[name, c0] = (g, c1)
+
+        def quant(name, c0):
+            g, c1 = grouped[name, c0]
+            codes = keep.tile([P, c1 - c0], U32, name="codes_%s_%d" % (name, c0), align_bytes=64)
+            scales = keep.tile([P, c1 - c0], U8, name="scales_%s_%d" % (name, c0), align_bytes=64)
+            nc.vector.quantize_mx(out=codes[:].bitcast(FP8X4), scales=scales[:], in_=g[:].rearrange("p n t -> p (n t)"))
+            for c in range(c0, c1, P):
+                quantised[name, c // P] = (codes[:, c - c0 : c - c0 + P], scales[:, c - c0 : c - c0 + P])
+
+        def mm(name, b):
+            codes, scales = quantised[name, b]
+            words, plane = moving[name]
+            nc.tensor.matmul_mx(
+                out=(gate_ps if name == "w3" else sum_ps)[b][:],
+                lhsT=codes.bitcast(FP8X4),
+                lhsT_scale=scales,
+                rhs=words[:].bitcast(FP8X4),
+                rhs_scale=plane,
+                start=name != "w2",
+                stop=name != "w1",
+            )
+
+        def sig(b):
+            nc.scalar.activation(gates[b][:], gate_ps[b][:], SIGMOID)
+
+        def finish(b):
+            res = keep.tile([P, S], F32, name="res%d" % b)
+            nc.vector.tensor_tensor(res[:], sum_ps[b][:], gates[b][:], MULT)
+            nc.sync.dma_start(out=out[b * P : (b + 1) * P, :], in_=res[:])
+
+        cast("s", "w3", 0, 256)
+        quant("w3", 0)
+        mm("w3", 0)
+        mm("w3", 1)
+        cast("s", "w3", 256, 512)
+        quant("w3", 256)
+        mm("w3", 2)
+        mm("w3", 3)
+        cast("v", "w1", 0, 256)
+        quant("w1", 0)
+        mm("w1", 0)
+        mm("w1", 1)
+        sig(0)
+        sig(1)
+        sig(2)
+        sig(3)
+        cast("v", "w2", 0, 256)
+        quant("w2", 0)
+        mm("w2", 0)
+        mm("w2", 1)
+        cast("s", "w1", 256, 512)
+        cast("v", "w2", 256, 384)
+        cast("s", "w2", 384, 512)
+        quant("w1", 256)
+        mm("w1", 2)
+        quant("w2", 256)
+        mm("w2", 2)
+        mm("w1", 3)
+        quant("w2", 384)
+        mm("w2", 3)
+        finish(0)
+        finish(1)
+        finish(2)
+        finish(3)

@@ -34,8 +34,8 @@ def tile_picked_ngramgate_none_p_kernel(tc, x_words, x_scales, w1, w2, w3, offs,
         nc.sync.dma_start(offs_sb[:], offs)
         nc.sync.dma_start(own_sb[:], own)
 
-        byte_table = keep.tile([P, T], U8, name="byte_table", tag="late", align_bytes=64)
-        nc.sync.dma_start(out=byte_table[:].bitcast(I32), in_=x_scales[0].bitcast(I32).unsqueeze(1).broadcast_to([16, 8, T // 4]))
+        byte_table = keep.tile([P, T], U8, name="byte_table", align_bytes=64)
+        nc.vector.memset(byte_table[:].bitcast(I32), 0)
         x_plane = keep.tile([P, 2 * S], U8, name="x_plane", align_bytes=64)
         nc.vector.memset(x_plane[:].bitcast(I32), 0)
         warm_in = keep.tile([P, 1], F32, name="warm_in")
@@ -47,16 +47,21 @@ def tile_picked_ngramgate_none_p_kernel(tc, x_words, x_scales, w1, w2, w3, offs,
         weights = {"w1": w1, "w2": w2, "w3": w3}
         raw = {}
 
-        def load(name, c0, c1):
+        def load(name, c0, c1, parts=1):
+            if name == "s":
+                nc.sync.dma_start(out=byte_table[0:P:8, :].bitcast(I32), in_=x_scales[0].bitcast(I32))
+                return
             if name == "x":
                 nc.sync.dma_start(out=word_table[:].bitcast(I32), in_=x_words[0].rearrange("p c r -> p (c r)").bitcast(I32))
                 return
             t = keep.tile([P, PACK, c1 - c0], F32, name="raw_%s_%d" % (name, c0))
-            nc.sync.dma_start(out=t[:], in_=weights[name][:, c0:c1].rearrange("(p j) n -> p j n", j=PACK))
+            for a in range(0, PACK, PACK // parts):
+                rows = slice(a, a + PACK // parts)
+                nc.sync.dma_start(out=t[:, rows, :], in_=weights[name][:, c0:c1].rearrange("(p j) n -> p j n", j=PACK)[:, rows, :])
             for c in range(c0, c1, P):
                 raw[name, c] = (t, c0)
 
-        for item in [("w3", 0, 256), ("x", 0, 0), ("w3", 256, 512)]:
+        for item in [("w3", 0, 256, 2), ("s", 0, 0), ("x", 0, 0), ("w1", 0, 256), ("w2", 0, 256), ("w3", 256, 512)]:
             load(*item)
 
         picked_bytes = keep.tile([P, 2 * S], U8, name="picked_bytes", align_bytes=64)
@@ -65,15 +70,17 @@ def tile_picked_ngramgate_none_p_kernel(tc, x_words, x_scales, w1, w2, w3, offs,
         for i in range(ROWS):
             nc.sync.dma_start(out=x_plane[i:P:QUAD, :].bitcast(I32), in_=picked_bytes[8 * i : P : QUAD, :].bitcast(I32))
 
-        late = [("w1", 0, 256), ("w2", 0, 256), ("w1", 256, 512), ("w2", 256, 384), ("w2", 384, 512)]
-        late_raw = keep.tile([P, PACK * sum(c1 - c0 for name, c0, c1 in late)], F32, name="late_raw", tag="late", align_bytes=64)
-        at = 0
-        for name, c0, c1 in late:
-            t = late_raw[:, at : at + PACK * (c1 - c0)].rearrange("p (j n) -> p j n", j=PACK)
-            nc.sync.dma_start(out=t, in_=weights[name][:, c0:c1].rearrange("(p j) n -> p j n", j=PACK))
-            for c in range(c0, c1, P):
-                raw[name, c] = (t, c0)
-            at = at + PACK * (c1 - c0)
+        def load_late():
+            late = [("w1", 256, 512), ("w2", 256, 384), ("w2", 384, 512)]
+            late_raw = keep.tile([P, PACK * sum(c1 - c0 for name, c0, c1 in late)], F32, name="late_raw", tag="late", align_bytes=64)
+            at = 0
+            for name, c0, c1 in late:
+                t = late_raw[:, at : at + PACK * (c1 - c0)].rearrange("p (j n) -> p j n", j=PACK)
+                nc.sync.dma_start(out=t, in_=weights[name][:, c0:c1].rearrange("(p j) n -> p j n", j=PACK))
+                for c in range(c0, c1, P):
+                    raw[name, c] = (t, c0)
+                at = at + PACK * (c1 - c0)
+            return late_raw[:, at - 1 : at]
 
         hashed = keep.tile([P, S], U32, name="hashed", align_bytes=64)
         mine = keep.tile([P, S], U32, name="mine", align_bytes=64)
@@ -87,13 +94,14 @@ def tile_picked_ngramgate_none_p_kernel(tc, x_words, x_scales, w1, w2, w3, offs,
 
         grouped = {}
         quantised = {}
+        whole = {}
         gate_ps = [psum.tile([P, S], F32, name="gate_ps%d" % b) for b in range(N // P)]
         sum_ps = [psum.tile([P, S], F32, name="sum_ps%d" % b) for b in range(N // P)]
-        gates = [keep.tile([P, S], F32, name="gate%d" % b) for b in range(N // P)]
+        gates = [keep.tile([P, S], F32, name="gate%d" % b)[:] for b in range(2)]
 
         def cast(engine, name, c0, c1):
             t, base = raw[name, c0]
-            g = keep.tile([P, c1 - c0, PACK], BF16, name="grouped_%s_%d" % (name, c0), align_bytes=64)
+            g = keep.tile([P, c1 - c0, PACK], BF16, name="grouped_%s_%d" % (name, c0), tag={("w3", 0): "late"}.get((name, c0), "grouped_%s_%d" % (name, c0)), align_bytes=64)
             dst = g[:].rearrange("p (c i) t -> p c t i", i=4)
             src = t[:, :, c0 - base : c1 - base].rearrange("p t (c i) -> p c t i", i=4)
             if engine == "s":
@@ -107,6 +115,7 @@ def tile_picked_ngramgate_none_p_kernel(tc, x_words, x_scales, w1, w2, w3, offs,
             codes = keep.tile([P, c1 - c0], U32, name="codes_%s_%d" % (name, c0), align_bytes=64)
             scales = keep.tile([P, c1 - c0], U8, name="scales_%s_%d" % (name, c0), align_bytes=64)
             nc.vector.quantize_mx(out=codes[:].bitcast(FP8X4), scales=scales[:], in_=g[:].rearrange("p n t -> p (n t)"))
+            whole[name, c0] = (codes, scales)
             for c in range(c0, c1, P):
                 quantised[name, c // P] = (codes[:, c - c0 : c - c0 + P], scales[:, c - c0 : c - c0 + P])
 
@@ -123,45 +132,66 @@ def tile_picked_ngramgate_none_p_kernel(tc, x_words, x_scales, w1, w2, w3, offs,
                 stop=name != "w1",
             )
 
-        def sig(b):
-            nc.scalar.activation(gates[b][:], gate_ps[b][:], SIGMOID)
+        def warm_pe(count):
+            codes, scales = whole["w3", 0]
+            for i in range(count):
+                nc.tensor.matmul_mx(
+                    out=sum_ps[3][:, 0:256],
+                    lhsT=codes[:, 0:P].bitcast(FP8X4),
+                    lhsT_scale=scales[:, 0:P],
+                    rhs=codes[:].bitcast(FP8X4),
+                    rhs_scale=scales[:],
+                    start=True,
+                    stop=True,
+                )
 
-        def finish(b):
-            res = keep.tile([P, S], F32, name="res%d" % b)
-            nc.vector.tensor_tensor(res[:], sum_ps[b][:], gates[b][:], MULT)
-            nc.sync.dma_start(out=out[b * P : (b + 1) * P, :], in_=res[:])
+        def late_gates():
+            both = keep.tile([P, 2 * S], F32, name="late_gates", tag="late", align_bytes=64)
+            gates.extend([both[:, 0:S], both[:, S : 2 * S]])
+
+        def sig(b):
+            nc.scalar.activation(gates[b], gate_ps[b][:], SIGMOID)
+
+        def finish_all():
+            res = keep.tile([P, 4 * S], F32, name="res")
+            for b, c0, c1 in [(0, 0, S), (1, 0, S), (2, 0, S), (3, 0, S // 2), (3, S // 2, S)]:
+                part = res[:, b * S + c0 : b * S + c1]
+                nc.vector.tensor_tensor(part, sum_ps[b][:, c0:c1], gates[b][:, c0:c1], MULT)
+                nc.sync.dma_start(out=out[b * P : (b + 1) * P, c0:c1], in_=part)
 
         cast("s", "w3", 0, 256)
         quant("w3", 0)
+        last = load_late()
+        warm_pe(6)
+        cast("s", "w1", 0, 256)
+        quant("w1", 0)
+        cast("s", "w2", 0, 256)
+        quant("w2", 0)
+        cast("v", "w3", 256, 384)
+        cast("s", "w3", 384, 512)
+        quant("w3", 256)
+        quant("w3", 384)
         mm("w3", 0)
         mm("w3", 1)
-        cast("s", "w3", 256, 512)
-        quant("w3", 256)
+        mm("w1", 0)
+        mm("w2", 0)
         mm("w3", 2)
         mm("w3", 3)
-        cast("v", "w1", 0, 256)
-        quant("w1", 0)
-        mm("w1", 0)
         mm("w1", 1)
+        mm("w2", 1)
         sig(0)
         sig(1)
-        sig(2)
-        sig(3)
-        cast("v", "w2", 0, 256)
-        quant("w2", 0)
-        mm("w2", 0)
-        mm("w2", 1)
-        cast("s", "w1", 256, 512)
+        cast("v", "w1", 256, 512)
         cast("v", "w2", 256, 384)
         cast("s", "w2", 384, 512)
         quant("w1", 256)
-        mm("w1", 2)
         quant("w2", 256)
+        quant("w2", 384)
+        mm("w1", 2)
         mm("w2", 2)
         mm("w1", 3)
-        quant("w2", 384)
         mm("w2", 3)
-        finish(0)
-        finish(1)
-        finish(2)
-        finish(3)
+        late_gates()
+        sig(2)
+        sig(3)
+        finish_all()

@@ -34,7 +34,7 @@ def tile_picked_ngramgate_none_p_kernel(tc, x_words, x_scales, w1, w2, w3, offs,
         nc.sync.dma_start(offs_sb[:], offs)
         nc.sync.dma_start(own_sb[:], own)
 
-        byte_table = keep.tile([P, T], U8, name="byte_table", align_bytes=64)
+        byte_table = keep.tile([P, T], U8, name="byte_table", tag="late", align_bytes=64)
         nc.vector.memset(byte_table[:].bitcast(I32), 0)
         x_plane = keep.tile([P, 2 * S], U8, name="x_plane", align_bytes=64)
         nc.vector.memset(x_plane[:].bitcast(I32), 0)
@@ -52,7 +52,7 @@ def tile_picked_ngramgate_none_p_kernel(tc, x_words, x_scales, w1, w2, w3, offs,
                 nc.sync.dma_start(out=byte_table[0:P:8, :].bitcast(I32), in_=x_scales[0].bitcast(I32))
                 return
             if name == "x":
-                nc.sync.dma_start(out=word_table[:].bitcast(I32), in_=x_words[0].rearrange("p c r -> p (c r)").bitcast(I32))
+                nc.sync.dma_start(out=word_table[:, c0:c1].bitcast(I32), in_=x_words[0, :, c0:c1, :].rearrange("p c r -> p (c r)").bitcast(I32))
                 return
             t = keep.tile([P, PACK, c1 - c0], F32, name="raw_%s_%d" % (name, c0))
             for a in range(0, PACK, PACK // parts):
@@ -61,7 +61,7 @@ def tile_picked_ngramgate_none_p_kernel(tc, x_words, x_scales, w1, w2, w3, offs,
             for c in range(c0, c1, P):
                 raw[name, c] = (t, c0)
 
-        for item in [("w3", 0, 256, 2), ("s", 0, 0), ("x", 0, 0), ("w1", 0, 256), ("w2", 0, 256), ("w3", 256, 512)]:
+        for item in [("x", 0, 256), ("x", 256, 512), ("s", 0, 0), ("w3", 0, 512), ("x", 512, 2048), ("w1", 0, 512)]:
             load(*item)
 
         picked_bytes = keep.tile([P, 2 * S], U8, name="picked_bytes", align_bytes=64)
@@ -71,7 +71,7 @@ def tile_picked_ngramgate_none_p_kernel(tc, x_words, x_scales, w1, w2, w3, offs,
             nc.sync.dma_start(out=x_plane[i:P:QUAD, :].bitcast(I32), in_=picked_bytes[8 * i : P : QUAD, :].bitcast(I32))
 
         def load_late():
-            late = [("w1", 256, 512), ("w2", 256, 384), ("w2", 384, 512)]
+            late = [("w2", 0, 256), ("w2", 256, 384), ("w2", 384, 512)]
             late_raw = keep.tile([P, PACK * sum(c1 - c0 for name, c0, c1 in late)], F32, name="late_raw", tag="late", align_bytes=64)
             at = 0
             for name, c0, c1 in late:
@@ -97,11 +97,11 @@ def tile_picked_ngramgate_none_p_kernel(tc, x_words, x_scales, w1, w2, w3, offs,
         whole = {}
         gate_ps = [psum.tile([P, S], F32, name="gate_ps%d" % b) for b in range(N // P)]
         sum_ps = [psum.tile([P, S], F32, name="sum_ps%d" % b) for b in range(N // P)]
-        gates = [keep.tile([P, S], F32, name="gate%d" % b)[:] for b in range(2)]
+        gates = [keep.tile([P, S], F32, name="gate%d" % b) for b in range(N // P)]
 
         def cast(engine, name, c0, c1):
             t, base = raw[name, c0]
-            g = keep.tile([P, c1 - c0, PACK], BF16, name="grouped_%s_%d" % (name, c0), tag={("w3", 0): "late"}.get((name, c0), "grouped_%s_%d" % (name, c0)), align_bytes=64)
+            g = keep.tile([P, c1 - c0, PACK], BF16, name="grouped_%s_%d" % (name, c0), tag={}.get((name, c0), "grouped_%s_%d" % (name, c0)), align_bytes=64)
             dst = g[:].rearrange("p (c i) t -> p c t i", i=4)
             src = t[:, :, c0 - base : c1 - base].rearrange("p t (c i) -> p c t i", i=4)
             if engine == "s":
@@ -145,12 +145,8 @@ def tile_picked_ngramgate_none_p_kernel(tc, x_words, x_scales, w1, w2, w3, offs,
                     stop=True,
                 )
 
-        def late_gates():
-            both = keep.tile([P, 2 * S], F32, name="late_gates", tag="late", align_bytes=64)
-            gates.extend([both[:, 0:S], both[:, S : 2 * S]])
-
         def sig(b):
-            nc.scalar.activation(gates[b], gate_ps[b][:], SIGMOID)
+            nc.scalar.activation(gates[b][:], gate_ps[b][:], SIGMOID)
 
         def finish_all():
             res = keep.tile([P, 4 * S], F32, name="res")
@@ -159,39 +155,38 @@ def tile_picked_ngramgate_none_p_kernel(tc, x_words, x_scales, w1, w2, w3, offs,
                 nc.vector.tensor_tensor(part, sum_ps[b][:, c0:c1], gates[b][:, c0:c1], MULT)
                 nc.sync.dma_start(out=out[b * P : (b + 1) * P, c0:c1], in_=part)
 
-        cast("s", "w3", 0, 256)
-        quant("w3", 0)
         last = load_late()
+        cast("s", "w3", 0, 256)
+        cast("v", "w3", 256, 512)
+        quant("w3", 0)
         warm_pe(6)
-        cast("s", "w1", 0, 256)
-        quant("w1", 0)
-        cast("s", "w2", 0, 256)
-        quant("w2", 0)
-        cast("v", "w3", 256, 384)
-        cast("s", "w3", 384, 512)
         quant("w3", 256)
-        quant("w3", 384)
         mm("w3", 0)
         mm("w3", 1)
-        mm("w1", 0)
-        mm("w2", 0)
         mm("w3", 2)
         mm("w3", 3)
+        cast("v", "w1", 0, 256)
+        cast("s", "w1", 256, 512)
+        quant("w1", 0)
+        mm("w1", 0)
         mm("w1", 1)
-        mm("w2", 1)
         sig(0)
+        cast("v", "w2", 0, 128)
+        cast("s", "w2", 128, 256)
+        quant("w1", 256)
+        quant("w2", 0)
+        quant("w2", 128)
+        mm("w2", 0)
+        mm("w2", 1)
         sig(1)
-        cast("v", "w1", 256, 512)
         cast("v", "w2", 256, 384)
         cast("s", "w2", 384, 512)
-        quant("w1", 256)
         quant("w2", 256)
         quant("w2", 384)
         mm("w1", 2)
         mm("w2", 2)
         mm("w1", 3)
         mm("w2", 3)
-        late_gates()
         sig(2)
         sig(3)
         finish_all()

@@ -17,10 +17,14 @@ MULT = mybir.AluOpType.mult
 
 P = 128
 PACK = 4
-QUAD = 32
-ROWS = 4
-SHIFT = 14
-SPAN = P - QUAD + ROWS
+GROUP = 16
+BLOCK_PARTITIONS = 8
+QUADRANT = 32
+PLANE_ROWS = QUADRANT // BLOCK_PARTITIONS
+HALF = N // 2
+LINE = 4
+FIRST_WORDS = 256
+WARM_PASSES = 6
 
 
 def tile_picked_ngramgate_none_p_kernel(tc, x_words, x_scales, w1, w2, w3, offs, own, out):
@@ -29,164 +33,136 @@ def tile_picked_ngramgate_none_p_kernel(tc, x_words, x_scales, w1, w2, w3, offs,
         keep = ctx.enter_context(tc.tile_pool(name="keep", bufs=1))
         psum = ctx.enter_context(tc.psum_pool(name="psum", bufs=1))
 
-        offs_sb = keep.tile([P, S // 16], U16, name="offs_sb")
-        own_sb = keep.tile([P, S // 16], U16, name="own_sb")
+        offs_sb = keep.tile([P, S // GROUP], U16, name="offs_sb")
+        own_sb = keep.tile([P, S // GROUP], U16, name="own_sb")
         nc.sync.dma_start(offs_sb[:], offs)
         nc.sync.dma_start(own_sb[:], own)
 
-        byte_table = keep.tile([P, T], U8, name="byte_table", tag="late", align_bytes=64)
+        byte_table = keep.tile([P, T], U8, name="byte_table", tag="shared", align_bytes=64)
         nc.vector.memset(byte_table[:].bitcast(I32), 0)
         x_plane = keep.tile([P, 2 * S], U8, name="x_plane", align_bytes=64)
         nc.vector.memset(x_plane[:].bitcast(I32), 0)
+
         warm_in = keep.tile([P, 1], F32, name="warm_in")
         warm_out = keep.tile([P, 1], F32, name="warm_out")
         nc.vector.memset(warm_in[:], 0.0)
         nc.scalar.activation(warm_out[:], warm_in[:], SIGMOID)
 
         word_table = keep.tile([P, T], U32, name="word_table", align_bytes=64)
-        weights = {"w1": w1, "w2": w2, "w3": w3}
-        raw = {}
 
-        def load(name, c0, c1, parts=1):
-            if name == "s":
-                nc.sync.dma_start(out=byte_table[0:P:8, :].bitcast(I32), in_=x_scales[0].bitcast(I32))
-                return
-            if name == "x":
-                nc.sync.dma_start(out=word_table[:, c0:c1].bitcast(I32), in_=x_words[0, :, c0:c1, :].rearrange("p c r -> p (c r)").bitcast(I32))
-                return
-            t = keep.tile([P, PACK, c1 - c0], F32, name="raw_%s_%d" % (name, c0))
-            for a in range(0, PACK, PACK // parts):
-                rows = slice(a, a + PACK // parts)
-                nc.sync.dma_start(out=t[:, rows, :], in_=weights[name][:, c0:c1].rearrange("(p j) n -> p j n", j=PACK)[:, rows, :])
-            for c in range(c0, c1, P):
-                raw[name, c] = (t, c0)
+        def load_words(c0, c1):
+            source = x_words[0, :, c0:c1, :].rearrange("p c r -> p (c r)").bitcast(I32)
+            nc.sync.dma_start(out=word_table[:, c0:c1].bitcast(I32), in_=source)
 
-        for item in [("x", 0, 256), ("x", 256, 512), ("s", 0, 0), ("w3", 0, 512), ("x", 512, 2048), ("w1", 0, 512)]:
-            load(*item)
+        def load_rows(tile_view, columns):
+            nc.sync.dma_start(out=tile_view, in_=columns.rearrange("(p j) n -> p j n", j=PACK))
+
+        load_words(0, FIRST_WORDS)
+        load_words(FIRST_WORDS, 2 * FIRST_WORDS)
+        nc.sync.dma_start(out=byte_table[0:P:BLOCK_PARTITIONS, :].bitcast(I32), in_=x_scales[0].bitcast(I32))
+        w3_raw = keep.tile([P, PACK, N], F32, name="w3_raw")
+        load_rows(w3_raw[:], w3)
+        load_words(2 * FIRST_WORDS, T)
+        w1_raw = keep.tile([P, PACK, N], F32, name="w1_raw")
+        load_rows(w1_raw[:], w1)
 
         picked_bytes = keep.tile([P, 2 * S], U8, name="picked_bytes", align_bytes=64)
         nc.vector.tensor_copy(picked_bytes[:, 0:S], byte_table[:].indirect(offs_sb[:]))
         nc.vector.tensor_copy(picked_bytes[:, S : 2 * S], byte_table[:].indirect(own_sb[:]))
-        for i in range(ROWS):
-            nc.sync.dma_start(out=x_plane[i:P:QUAD, :].bitcast(I32), in_=picked_bytes[8 * i : P : QUAD, :].bitcast(I32))
-
-        def load_late():
-            late = [("w2", 0, 256), ("w2", 256, 384), ("w2", 384, 512)]
-            late_raw = keep.tile([P, PACK * sum(c1 - c0 for name, c0, c1 in late)], F32, name="late_raw", tag="late", align_bytes=64)
-            at = 0
-            for name, c0, c1 in late:
-                t = late_raw[:, at : at + PACK * (c1 - c0)].rearrange("p (j n) -> p j n", j=PACK)
-                nc.sync.dma_start(out=t, in_=weights[name][:, c0:c1].rearrange("(p j) n -> p j n", j=PACK))
-                for c in range(c0, c1, P):
-                    raw[name, c] = (t, c0)
-                at = at + PACK * (c1 - c0)
-            return late_raw[:, at - 1 : at]
-
-        hashed = keep.tile([P, S], U32, name="hashed", align_bytes=64)
-        mine = keep.tile([P, S], U32, name="mine", align_bytes=64)
-        nc.vector.tensor_copy(hashed[:], word_table[:].indirect(offs_sb[:]))
-        nc.vector.tensor_copy(mine[:], word_table[:].indirect(own_sb[:]))
-        moving = {
-            "w1": (hashed, x_plane[:, 0:S]),
-            "w3": (hashed, x_plane[:, 0:S]),
-            "w2": (mine, x_plane[:, S : 2 * S]),
-        }
-
-        grouped = {}
-        quantised = {}
-        whole = {}
-        gate_ps = [psum.tile([P, S], F32, name="gate_ps%d" % b) for b in range(N // P)]
-        sum_ps = [psum.tile([P, S], F32, name="sum_ps%d" % b) for b in range(N // P)]
-        gates = [keep.tile([P, S], F32, name="gate%d" % b) for b in range(N // P)]
-
-        def cast(engine, name, c0, c1):
-            t, base = raw[name, c0]
-            g = keep.tile([P, c1 - c0, PACK], BF16, name="grouped_%s_%d" % (name, c0), tag={}.get((name, c0), "grouped_%s_%d" % (name, c0)), align_bytes=64)
-            dst = g[:].rearrange("p (c i) t -> p c t i", i=4)
-            src = t[:, :, c0 - base : c1 - base].rearrange("p t (c i) -> p c t i", i=4)
-            if engine == "s":
-                nc.scalar.copy(dst, src)
-            else:
-                nc.vector.tensor_copy(dst, src)
-            grouped[name, c0] = (g, c1)
-
-        def quant(name, c0):
-            g, c1 = grouped[name, c0]
-            codes = keep.tile([P, c1 - c0], U32, name="codes_%s_%d" % (name, c0), align_bytes=64)
-            scales = keep.tile([P, c1 - c0], U8, name="scales_%s_%d" % (name, c0), align_bytes=64)
-            nc.vector.quantize_mx(out=codes[:].bitcast(FP8X4), scales=scales[:], in_=g[:].rearrange("p n t -> p (n t)"))
-            whole[name, c0] = (codes, scales)
-            for c in range(c0, c1, P):
-                quantised[name, c // P] = (codes[:, c - c0 : c - c0 + P], scales[:, c - c0 : c - c0 + P])
-
-        def mm(name, b):
-            codes, scales = quantised[name, b]
-            words, plane = moving[name]
-            nc.tensor.matmul_mx(
-                out=(gate_ps if name == "w3" else sum_ps)[b][:],
-                lhsT=codes.bitcast(FP8X4),
-                lhsT_scale=scales,
-                rhs=words[:].bitcast(FP8X4),
-                rhs_scale=plane,
-                start=name != "w2",
-                stop=name != "w1",
+        for i in range(PLANE_ROWS):
+            nc.sync.dma_start(
+                out=x_plane[i:P:QUADRANT, :].bitcast(I32),
+                in_=picked_bytes[BLOCK_PARTITIONS * i : P : QUADRANT, :].bitcast(I32),
             )
 
-        def warm_pe(count):
-            codes, scales = whole["w3", 0]
-            for i in range(count):
-                nc.tensor.matmul_mx(
-                    out=sum_ps[3][:, 0:256],
-                    lhsT=codes[:, 0:P].bitcast(FP8X4),
-                    lhsT_scale=scales[:, 0:P],
-                    rhs=codes[:].bitcast(FP8X4),
-                    rhs_scale=scales[:],
-                    start=True,
-                    stop=True,
-                )
+        hashed_words = keep.tile([P, S], U32, name="hashed_words", align_bytes=64)
+        own_words = keep.tile([P, S], U32, name="own_words", align_bytes=64)
+        nc.vector.tensor_copy(hashed_words[:], word_table[:].indirect(offs_sb[:]))
+        nc.vector.tensor_copy(own_words[:], word_table[:].indirect(own_sb[:]))
+        x_hashed = (hashed_words[:], x_plane[:, 0:S])
+        x_own = (own_words[:], x_plane[:, S : 2 * S])
 
-        def sig(b):
-            nc.scalar.activation(gates[b][:], gate_ps[b][:], SIGMOID)
+        gate_ps = [psum.tile([P, S], F32, name="gate_ps%d" % b) for b in range(N // P)]
+        sum_ps = [psum.tile([P, S], F32, name="sum_ps%d" % b) for b in range(N // P)]
+        gates = [keep.tile([P, S], F32, name="gate%d" % b)[:] for b in range(HALF // P)]
 
-        def finish_all():
-            res = keep.tile([P, 4 * S], F32, name="res")
-            for b, c0, c1 in [(0, 0, S), (1, 0, S), (2, 0, S), (3, 0, S // 2), (3, S // 2, S)]:
-                part = res[:, b * S + c0 : b * S + c1]
-                nc.vector.tensor_tensor(part, sum_ps[b][:, c0:c1], gates[b][:, c0:c1], MULT)
-                nc.sync.dma_start(out=out[b * P : (b + 1) * P, c0:c1], in_=part)
+        w2_raw = keep.tile([P, PACK * N], F32, name="w2_raw", tag="shared", align_bytes=64)
+        w2_pieces = []
+        for c0, c1 in ((0, HALF), (HALF, HALF + P), (HALF + P, N)):
+            piece = w2_raw[:, PACK * c0 : PACK * c1].rearrange("p (j n) -> p j n", j=PACK)
+            load_rows(piece, w2[:, c0:c1])
+            w2_pieces.append(piece)
 
-        last = load_late()
-        cast("s", "w3", 0, 256)
-        cast("v", "w3", 256, 512)
-        quant("w3", 0)
-        warm_pe(6)
-        quant("w3", 256)
-        mm("w3", 0)
-        mm("w3", 1)
-        mm("w3", 2)
-        mm("w3", 3)
-        cast("v", "w1", 0, 256)
-        cast("s", "w1", 256, 512)
-        quant("w1", 0)
-        mm("w1", 0)
-        mm("w1", 1)
-        sig(0)
-        cast("v", "w2", 0, 128)
-        cast("s", "w2", 128, 256)
-        quant("w1", 256)
-        quant("w2", 0)
-        quant("w2", 128)
-        mm("w2", 0)
-        mm("w2", 1)
-        sig(1)
-        cast("v", "w2", 256, 384)
-        cast("s", "w2", 384, 512)
-        quant("w2", 256)
-        quant("w2", 384)
-        mm("w1", 2)
-        mm("w2", 2)
-        mm("w1", 3)
-        mm("w2", 3)
-        sig(2)
-        sig(3)
-        finish_all()
+        def interleave(copy, name, raw):
+            grouped = keep.tile([P, raw.shape[2], PACK], BF16, name=name + "_grouped", align_bytes=64)
+            copy(grouped[:].rearrange("p (c i) t -> p c t i", i=LINE), raw.rearrange("p t (c i) -> p c t i", i=LINE))
+            return grouped
+
+        def quantise(name, grouped):
+            width = grouped.shape[1]
+            words = keep.tile([P, width], U32, name=name + "_words", align_bytes=64)
+            plane = keep.tile([P, width], U8, name=name + "_plane", align_bytes=64)
+            nc.vector.quantize_mx(out=words[:].bitcast(FP8X4), scales=plane[:], in_=grouped[:].rearrange("p n t -> p (n t)"))
+            return words[:], plane[:]
+
+        def multiply(bank, weights, c0, moving, start, stop):
+            nc.tensor.matmul_mx(
+                out=bank,
+                lhsT=weights[0][:, c0 : c0 + P].bitcast(FP8X4),
+                lhsT_scale=weights[1][:, c0 : c0 + P],
+                rhs=moving[0].bitcast(FP8X4),
+                rhs_scale=moving[1],
+                start=start,
+                stop=stop,
+            )
+
+        def make_gate(b):
+            nc.scalar.activation(gates[b], gate_ps[b][:], SIGMOID)
+
+        on_scalar, on_vector = nc.scalar.copy, nc.vector.tensor_copy
+
+        w3_low_grouped = interleave(on_scalar, "w3_low", w3_raw[:, :, 0:HALF])
+        w3_high_grouped = interleave(on_vector, "w3_high", w3_raw[:, :, HALF:N])
+        w3_low = quantise("w3_low", w3_low_grouped)
+        for warm_pass in range(WARM_PASSES):
+            multiply(sum_ps[N // P - 1][:, 0:HALF], w3_low, 0, w3_low, True, True)
+        w3_high = quantise("w3_high", w3_high_grouped)
+        for b in range(N // P):
+            multiply(gate_ps[b][:], w3_low if b * P < HALF else w3_high, b * P % HALF, x_hashed, True, True)
+
+        w1_low_grouped = interleave(on_vector, "w1_low", w1_raw[:, :, 0:HALF])
+        w1_high_grouped = interleave(on_scalar, "w1_high", w1_raw[:, :, HALF:N])
+        w1_low = quantise("w1_low", w1_low_grouped)
+        for b in (0, 1):
+            multiply(sum_ps[b][:], w1_low, b * P, x_hashed, True, False)
+        make_gate(0)
+
+        w2_grouped = [
+            interleave(on_vector, "w2_0", w2_pieces[0][:, :, 0:P]),
+            interleave(on_scalar, "w2_1", w2_pieces[0][:, :, P:HALF]),
+        ]
+        w1_high = quantise("w1_high", w1_high_grouped)
+        w2_blocks = [quantise("w2_%d" % b, w2_grouped[b]) for b in (0, 1)]
+        for b in (0, 1):
+            multiply(sum_ps[b][:], w2_blocks[b], 0, x_own, False, True)
+        make_gate(1)
+
+        w2_grouped.append(interleave(on_vector, "w2_2", w2_pieces[1]))
+        w2_grouped.append(interleave(on_scalar, "w2_3", w2_pieces[2]))
+        w2_blocks.extend([quantise("w2_%d" % b, w2_grouped[b]) for b in (2, 3)])
+        for b in (2, 3):
+            multiply(sum_ps[b][:], w1_high, b * P - HALF, x_hashed, True, False)
+            multiply(sum_ps[b][:], w2_blocks[b], 0, x_own, False, True)
+
+        late_gates = keep.tile([P, 2 * S], F32, name="late_gates", tag="shared", align_bytes=64)
+        gates.extend([late_gates[:, 0:S], late_gates[:, S : 2 * S]])
+        make_gate(2)
+        make_gate(3)
+
+        results = keep.tile([P, N // P * S], F32, name="results")
+        last = N // P - 1
+        pieces = [(b, 0, S) for b in range(last)] + [(last, 0, S // 2), (last, S // 2, S)]
+        for b, c0, c1 in pieces:
+            result = results[:, b * S + c0 : b * S + c1]
+            nc.vector.tensor_tensor(result, sum_ps[b][:, c0:c1], gates[b][:, c0:c1], MULT)
+            nc.sync.dma_start(out=out[b * P : (b + 1) * P, c0:c1], in_=result)

@@ -23,8 +23,6 @@ QUADRANT = 32
 PLANE_ROWS = QUADRANT // BLOCK_PARTITIONS
 HALF = N // 2
 LINE = 4
-FIRST_WORDS = 256
-WARM_PASSES = 6
 
 
 def tile_picked_ngramgate_none_p_kernel(tc, x_words, x_scales, w1, w2, w3, offs, own, out):
@@ -33,38 +31,51 @@ def tile_picked_ngramgate_none_p_kernel(tc, x_words, x_scales, w1, w2, w3, offs,
         keep = ctx.enter_context(tc.tile_pool(name="keep", bufs=1))
         psum = ctx.enter_context(tc.psum_pool(name="psum", bufs=1))
 
+        weights = {"w1": w1, "w2": w2, "w3": w3}
+        raw = {}
+
+        def load(name, first, count, queue):
+            tag = "%s_%d_raw" % (name, first)
+            tile = keep.tile([P, PACK, count * P], F32, name=tag, tag=tag, align_bytes=64)
+            columns = weights[name][:, first * P : (first + count) * P]
+            queue.dma_start(out=tile[:], in_=columns.rearrange("(p j) n -> p j n", j=PACK))
+            for b in range(count):
+                raw[name, first + b] = (tile, b * P)
+
         offs_sb = keep.tile([P, S // GROUP], U16, name="offs_sb")
         own_sb = keep.tile([P, S // GROUP], U16, name="own_sb")
-        nc.sync.dma_start(offs_sb[:], offs)
-        nc.sync.dma_start(own_sb[:], own)
-
-        byte_table = keep.tile([P, T], U8, name="byte_table", tag="shared", align_bytes=64)
+        byte_table = keep.tile([P, T], U8, name="byte_table", align_bytes=64)
         nc.vector.memset(byte_table[:].bitcast(I32), 0)
         x_plane = keep.tile([P, 2 * S], U8, name="x_plane", align_bytes=64)
         nc.vector.memset(x_plane[:].bitcast(I32), 0)
-
-        warm_in = keep.tile([P, 1], F32, name="warm_in")
-        warm_out = keep.tile([P, 1], F32, name="warm_out")
-        nc.vector.memset(warm_in[:], 0.0)
-        nc.scalar.activation(warm_out[:], warm_in[:], SIGMOID)
-
         word_table = keep.tile([P, T], U32, name="word_table", align_bytes=64)
+
+        def load_scales(queue):
+            queue.dma_start(out=byte_table[0:P:BLOCK_PARTITIONS, :].bitcast(I32), in_=x_scales[0].bitcast(I32))
 
         def load_words(c0, c1):
             source = x_words[0, :, c0:c1, :].rearrange("p c r -> p (c r)").bitcast(I32)
             nc.sync.dma_start(out=word_table[:, c0:c1].bitcast(I32), in_=source)
 
-        def load_rows(tile_view, columns):
-            nc.sync.dma_start(out=tile_view, in_=columns.rearrange("(p j) n -> p j n", j=PACK))
+        w1_tile = keep.tile([P, PACK, N], F32, name="w1_0_raw", tag="w1_0_raw", align_bytes=64)
+        for b in range(N // P):
+            raw["w1", b] = (w1_tile, b * P)
 
-        load_words(0, FIRST_WORDS)
-        load_words(FIRST_WORDS, 2 * FIRST_WORDS)
-        nc.sync.dma_start(out=byte_table[0:P:BLOCK_PARTITIONS, :].bitcast(I32), in_=x_scales[0].bitcast(I32))
-        w3_raw = keep.tile([P, PACK, N], F32, name="w3_raw")
-        load_rows(w3_raw[:], w3)
-        load_words(2 * FIRST_WORDS, T)
-        w1_raw = keep.tile([P, PACK, N], F32, name="w1_raw")
-        load_rows(w1_raw[:], w1)
+        def load_w1_rows(j0, j1):
+            nc.sync.dma_start(out=w1_tile[:, j0:j1, :], in_=w1.rearrange("(p j) n -> p j n", j=PACK)[:, j0:j1, :])
+
+        load_words(0, 512)
+        nc.sync.dma_start(offs_sb[:], offs)
+        load_scales(nc.sync)
+        nc.sync.dma_start(own_sb[:], own)
+        load("w3", 0, 4, nc.sync)
+        load_words(512, T)
+        load_w1_rows(0, 2)
+
+        warm_in = keep.tile([P, 1], F32, name="warm_in")
+        warm_out = keep.tile([P, 1], F32, name="warm_out")
+        nc.vector.memset(warm_in[:], 0.0)
+        nc.scalar.activation(warm_out[:], warm_in[:], SIGMOID)
 
         picked_bytes = keep.tile([P, 2 * S], U8, name="picked_bytes", align_bytes=64)
         nc.vector.tensor_copy(picked_bytes[:, 0:S], byte_table[:].indirect(offs_sb[:]))
@@ -74,95 +85,104 @@ def tile_picked_ngramgate_none_p_kernel(tc, x_words, x_scales, w1, w2, w3, offs,
                 out=x_plane[i:P:QUADRANT, :].bitcast(I32),
                 in_=picked_bytes[BLOCK_PARTITIONS * i : P : QUADRANT, :].bitcast(I32),
             )
+        load_w1_rows(2, 4)
+        load("w2", 0, 2, nc.sync)
+        load("w2", 2, 1, nc.sync)
+        load("w2", 3, 1, nc.sync)
 
+        gate_ps = [psum.tile([P, S], F32, name="gate_ps%d" % b) for b in range(N // P)]
+        sum_ps = [psum.tile([P, S], F32, name="sum_ps%d" % b) for b in range(N // P)]
+        results = {}
+        on_scalar, on_vector = nc.scalar.copy, nc.vector.tensor_copy
+        quantised = {}
+        gates = {}
+
+        def grouped_tile(name, first, count):
+            label = "%s_%d_grouped" % (name, first)
+            return keep.tile([P, count * P, PACK], BF16, name=label, tag=label, align_bytes=64)
+
+        def interleave(copy, grouped, place, name, first, count):
+            tile, c0 = raw[name, first]
+            source = tile[:, :, c0 : c0 + count * P]
+            target = grouped[:, place * P : (place + count) * P, :]
+            copy(target.rearrange("p (c i) t -> p c t i", i=LINE), source.rearrange("p t (c i) -> p c t i", i=LINE))
+
+        def quantise(grouped, name, first):
+            count = grouped.shape[1] // P
+            label = "%s_%d" % (name, first)
+            words = keep.tile([P, count * P], U32, name=label + "_words", align_bytes=64)
+            plane = keep.tile([P, count * P], U8, name=label + "_plane", align_bytes=64)
+            nc.vector.quantize_mx(out=words[:].bitcast(FP8X4), scales=plane[:], in_=grouped[:].rearrange("p n t -> p (n t)"))
+            for b in range(count):
+                quantised[name, first + b] = (words[:, b * P : (b + 1) * P], plane[:, b * P : (b + 1) * P])
+
+        def multiply(key):
+            name, b = key
+            words, plane = quantised[key]
+            moving = x_own if name == "w2" else x_hashed
+            nc.tensor.matmul_mx(
+                out=(gate_ps if name == "w3" else sum_ps)[b][:],
+                lhsT=words.bitcast(FP8X4),
+                lhsT_scale=plane,
+                rhs=moving[0].bitcast(FP8X4),
+                rhs_scale=moving[1],
+                start=name != "w2",
+                stop=name != "w1",
+            )
+
+        def make_gates(blocks, tag, last_pieces=1):
+            tile = keep.tile([P, len(blocks), S], F32, name="gate%d" % blocks[0], tag=tag, align_bytes=64)
+            for place, b in enumerate(blocks):
+                gates[b] = tile[:, place, :]
+                pieces = last_pieces if b == blocks[-1] else 1
+                for piece in range(pieces):
+                    columns = slice(piece * S // pieces, (piece + 1) * S // pieces)
+                    nc.scalar.activation(gates[b][:, columns], gate_ps[b][:, columns], SIGMOID)
+
+        def finish(b, tag, pieces=1):
+            result = keep.tile([P, S], F32, name="result%d" % b, tag=tag, align_bytes=64)
+            results[b] = result
+            for piece in range(pieces):
+                columns = slice(piece * S // pieces, (piece + 1) * S // pieces)
+                nc.vector.tensor_tensor(result[:, columns], sum_ps[b][:, columns], gates[b][:, columns], MULT)
+                nc.sync.dma_start(out=out[b * P : (b + 1) * P, columns], in_=result[:, columns])
+
+        w3_low, w3_high = grouped_tile("w3", 0, 2), grouped_tile("w3", 2, 2)
+        interleave(on_scalar, w3_low, 0, "w3", 0, 1)
+        interleave(on_vector, w3_low, 1, "w3", 1, 1)
+        interleave(on_vector, w3_high, 0, "w3", 2, 2)
+        quantise(w3_low, "w3", 0)
+        quantise(w3_high, "w3", 2)
         hashed_words = keep.tile([P, S], U32, name="hashed_words", align_bytes=64)
         own_words = keep.tile([P, S], U32, name="own_words", align_bytes=64)
         nc.vector.tensor_copy(hashed_words[:], word_table[:].indirect(offs_sb[:]))
         nc.vector.tensor_copy(own_words[:], word_table[:].indirect(own_sb[:]))
         x_hashed = (hashed_words[:], x_plane[:, 0:S])
         x_own = (own_words[:], x_plane[:, S : 2 * S])
-
-        gate_ps = [psum.tile([P, S], F32, name="gate_ps%d" % b) for b in range(N // P)]
-        sum_ps = [psum.tile([P, S], F32, name="sum_ps%d" % b) for b in range(N // P)]
-        gates = [keep.tile([P, S], F32, name="gate%d" % b)[:] for b in range(HALF // P)]
-
-        w2_raw = keep.tile([P, PACK * N], F32, name="w2_raw", tag="shared", align_bytes=64)
-        w2_pieces = []
-        for c0, c1 in ((0, HALF), (HALF, HALF + P), (HALF + P, N)):
-            piece = w2_raw[:, PACK * c0 : PACK * c1].rearrange("p (j n) -> p j n", j=PACK)
-            load_rows(piece, w2[:, c0:c1])
-            w2_pieces.append(piece)
-
-        def interleave(copy, name, raw):
-            grouped = keep.tile([P, raw.shape[2], PACK], BF16, name=name + "_grouped", align_bytes=64)
-            copy(grouped[:].rearrange("p (c i) t -> p c t i", i=LINE), raw.rearrange("p t (c i) -> p c t i", i=LINE))
-            return grouped
-
-        def quantise(name, grouped):
-            width = grouped.shape[1]
-            words = keep.tile([P, width], U32, name=name + "_words", align_bytes=64)
-            plane = keep.tile([P, width], U8, name=name + "_plane", align_bytes=64)
-            nc.vector.quantize_mx(out=words[:].bitcast(FP8X4), scales=plane[:], in_=grouped[:].rearrange("p n t -> p (n t)"))
-            return words[:], plane[:]
-
-        def multiply(bank, weights, c0, moving, start, stop):
-            nc.tensor.matmul_mx(
-                out=bank,
-                lhsT=weights[0][:, c0 : c0 + P].bitcast(FP8X4),
-                lhsT_scale=weights[1][:, c0 : c0 + P],
-                rhs=moving[0].bitcast(FP8X4),
-                rhs_scale=moving[1],
-                start=start,
-                stop=stop,
-            )
-
-        def make_gate(b):
-            nc.scalar.activation(gates[b], gate_ps[b][:], SIGMOID)
-
-        on_scalar, on_vector = nc.scalar.copy, nc.vector.tensor_copy
-
-        w3_low_grouped = interleave(on_scalar, "w3_low", w3_raw[:, :, 0:HALF])
-        w3_high_grouped = interleave(on_vector, "w3_high", w3_raw[:, :, HALF:N])
-        w3_low = quantise("w3_low", w3_low_grouped)
-        for warm_pass in range(WARM_PASSES):
-            multiply(sum_ps[N // P - 1][:, 0:HALF], w3_low, 0, w3_low, True, True)
-        w3_high = quantise("w3_high", w3_high_grouped)
         for b in range(N // P):
-            multiply(gate_ps[b][:], w3_low if b * P < HALF else w3_high, b * P % HALF, x_hashed, True, True)
-
-        w1_low_grouped = interleave(on_vector, "w1_low", w1_raw[:, :, 0:HALF])
-        w1_high_grouped = interleave(on_scalar, "w1_high", w1_raw[:, :, HALF:N])
-        w1_low = quantise("w1_low", w1_low_grouped)
-        for b in (0, 1):
-            multiply(sum_ps[b][:], w1_low, b * P, x_hashed, True, False)
-        make_gate(0)
-
-        w2_grouped = [
-            interleave(on_vector, "w2_0", w2_pieces[0][:, :, 0:P]),
-            interleave(on_scalar, "w2_1", w2_pieces[0][:, :, P:HALF]),
-        ]
-        w1_high = quantise("w1_high", w1_high_grouped)
-        w2_blocks = [quantise("w2_%d" % b, w2_grouped[b]) for b in (0, 1)]
-        for b in (0, 1):
-            multiply(sum_ps[b][:], w2_blocks[b], 0, x_own, False, True)
-        make_gate(1)
-
-        w2_grouped.append(interleave(on_vector, "w2_2", w2_pieces[1]))
-        w2_grouped.append(interleave(on_scalar, "w2_3", w2_pieces[2]))
-        w2_blocks.extend([quantise("w2_%d" % b, w2_grouped[b]) for b in (2, 3)])
-        for b in (2, 3):
-            multiply(sum_ps[b][:], w1_high, b * P - HALF, x_hashed, True, False)
-            multiply(sum_ps[b][:], w2_blocks[b], 0, x_own, False, True)
-
-        late_gates = keep.tile([P, 2 * S], F32, name="late_gates", tag="shared", align_bytes=64)
-        gates.extend([late_gates[:, 0:S], late_gates[:, S : 2 * S]])
-        make_gate(2)
-        make_gate(3)
-
-        results = keep.tile([P, N // P * S], F32, name="results")
-        last = N // P - 1
-        pieces = [(b, 0, S) for b in range(last)] + [(last, 0, S // 2), (last, S // 2, S)]
-        for b, c0, c1 in pieces:
-            result = results[:, b * S + c0 : b * S + c1]
-            nc.vector.tensor_tensor(result, sum_ps[b][:, c0:c1], gates[b][:, c0:c1], MULT)
-            nc.sync.dma_start(out=out[b * P : (b + 1) * P, c0:c1], in_=result)
+            multiply(("w3", b))
+        w1_low, w1_high = grouped_tile("w1", 0, 2), grouped_tile("w1", 2, 2)
+        w2_grouped = [grouped_tile("w2", b, 1) for b in range(N // P)]
+        interleave(on_vector, w1_low, 0, "w1", 0, 2)
+        interleave(on_scalar, w1_high, 0, "w1", 2, 1)
+        interleave(on_scalar, w1_high, 1, "w1", 3, 1)
+        quantise(w1_low, "w1", 0)
+        make_gates([0], "w1_0_raw")
+        interleave(on_vector, w2_grouped[0], 0, "w2", 0, 1)
+        interleave(on_scalar, w2_grouped[1], 0, "w2", 1, 1)
+        quantise(w1_high, "w1", 2)
+        quantise(w2_grouped[0], "w2", 0)
+        make_gates([1], "w2_0_raw")
+        interleave(on_vector, w2_grouped[2], 0, "w2", 2, 1)
+        interleave(on_scalar, w2_grouped[3], 0, "w2", 3, 1)
+        quantise(w2_grouped[1], "w2", 1)
+        quantise(w2_grouped[2], "w2", 2)
+        for key in (("w1", 0), ("w1", 1), ("w2", 0), ("w1", 2), ("w2", 1), ("w1", 3), ("w2", 2)):
+            multiply(key)
+        finish(0, "w2_2_grouped")
+        quantise(w2_grouped[3], "w2", 3)
+        multiply(("w2", 3))
+        make_gates([2, 3], "w2_3_raw", 2)
+        finish(1, "w2_3_grouped")
+        finish(2, "result2")
+        finish(3, "result3", 2)

@@ -22,7 +22,7 @@ BLOCK_PARTITIONS = 8
 QUADRANT = 32
 PLANE_ROWS = QUADRANT // BLOCK_PARTITIONS
 HALF = N // 2
-LINE = 4
+LINE = 2
 
 
 def tile_picked_ngramgate_none_p_kernel(tc, x_words, x_scales, w1, w2, w3, offs, own, out):

@@ -179,10 +179,10 @@ def tile_picked_ngramgate_none_p_kernel(tc, x_words, x_scales, w1, w2, w3, offs,
         quantise(w2_grouped[2], "w2", 2)
         for key in (("w1", 0), ("w1", 1), ("w2", 0), ("w1", 2), ("w2", 1), ("w1", 3), ("w2", 2)):
             multiply(key)
-        finish(0, "w2_2_grouped")
+        finish(0, "w2_2_grouped", 2)
         quantise(w2_grouped[3], "w2", 3)
         multiply(("w2", 3))
         make_gates([2, 3], "w2_3_raw", 2)
-        finish(1, "w2_3_grouped")
-        finish(2, "result2")
+        finish(1, "w2_3_grouped", 2)
+        finish(2, "result2", 2)
         finish(3, "result3", 2)

@@ -66,8 +66,8 @@ def tile_picked_ngramgate_none_p_kernel(tc, x_words, x_scales, w1, w2, w3, offs,
 
         load_words(0, 512)
         nc.sync.dma_start(offs_sb[:], offs)
-        load_scales(nc.sync)
         nc.sync.dma_start(own_sb[:], own)
+        load_scales(nc.sync)
         load("w3", 0, 4, nc.sync)
         load_words(512, T)
         load_w1_rows(0, 2)
@@ -90,8 +90,9 @@ def tile_picked_ngramgate_none_p_kernel(tc, x_words, x_scales, w1, w2, w3, offs,
         load("w2", 2, 1, nc.sync)
         load("w2", 3, 1, nc.sync)
 
-        gate_ps = [psum.tile([P, S], F32, name="gate_ps%d" % b) for b in range(N // P)]
-        sum_ps = [psum.tile([P, S], F32, name="sum_ps%d" % b) for b in range(N // P)]
+        gate_ps = [psum.tile([P, S], F32, name="gate_ps%d" % b, tag="gate_ps%d" % b) for b in range(N // P)]
+        sums = {}
+        banks = {}
         results = {}
         on_scalar, on_vector = nc.scalar.copy, nc.vector.tensor_copy
         quantised = {}
@@ -116,36 +117,49 @@ def tile_picked_ngramgate_none_p_kernel(tc, x_words, x_scales, w1, w2, w3, offs,
             for b in range(count):
                 quantised[name, first + b] = (words[:, b * P : (b + 1) * P], plane[:, b * P : (b + 1) * P])
 
-        def multiply(key):
+        def multiply(key, half=None):
             name, b = key
             words, plane = quantised[key]
             moving = x_own if name == "w2" else x_hashed
+            columns = slice(0, S) if half is None else slice(half * S // 2, (half + 1) * S // 2)
             nc.tensor.matmul_mx(
-                out=(gate_ps if name == "w3" else sum_ps)[b][:],
+                out=gate_ps[b][:] if name == "w3" else banks[b, half],
                 lhsT=words.bitcast(FP8X4),
                 lhsT_scale=plane,
-                rhs=moving[0].bitcast(FP8X4),
-                rhs_scale=moving[1],
+                rhs=moving[0][:, columns].bitcast(FP8X4),
+                rhs_scale=moving[1][:, columns],
                 start=name != "w2",
                 stop=name != "w1",
             )
 
-        def make_gates(blocks, tag, last_pieces=1):
+        def whole_bank(b, tag):
+            bank = psum.tile([P, S], F32, name="sum_ps%d" % b, tag=tag)
+            banks[b, None] = bank[:]
+            for half in (0, 1):
+                sums[b, half] = bank[:, half * S // 2 : (half + 1) * S // 2]
+
+        def two_banks(b):
+            for half in (0, 1):
+                bank = psum.tile([P, S], F32, name="sum_ps%d_%d" % (b, half))
+                banks[b, half] = bank[:, 0 : S // 2]
+                sums[b, half] = bank[:, 0 : S // 2]
+
+        def make_gates(blocks, tag, pieces):
             tile = keep.tile([P, len(blocks), S], F32, name="gate%d" % blocks[0], tag=tag, align_bytes=64)
             for place, b in enumerate(blocks):
                 gates[b] = tile[:, place, :]
-                pieces = last_pieces if b == blocks[-1] else 1
-                for piece in range(pieces):
-                    columns = slice(piece * S // pieces, (piece + 1) * S // pieces)
+                count = pieces if b == blocks[-1] else 1
+                for piece in range(count):
+                    columns = slice(piece * S // count, (piece + 1) * S // count)
                     nc.scalar.activation(gates[b][:, columns], gate_ps[b][:, columns], SIGMOID)
 
-        def finish(b, tag, pieces=1):
-            result = keep.tile([P, S], F32, name="result%d" % b, tag=tag, align_bytes=64)
-            results[b] = result
-            for piece in range(pieces):
-                columns = slice(piece * S // pieces, (piece + 1) * S // pieces)
-                nc.vector.tensor_tensor(result[:, columns], sum_ps[b][:, columns], gates[b][:, columns], MULT)
-                nc.sync.dma_start(out=out[b * P : (b + 1) * P, columns], in_=result[:, columns])
+        def finish(b, half, tag=None):
+            name = "result%d_%d" % (b, half)
+            columns = slice(half * S // 2, (half + 1) * S // 2)
+            result = keep.tile([P, S // 2], F32, name=name, tag=tag or name, align_bytes=64)
+            results[b, half] = result
+            nc.vector.tensor_tensor(result[:], sums[b, half], gates[b][:, columns], MULT)
+            nc.sync.dma_start(out=out[b * P : (b + 1) * P, columns], in_=result[:])
 
         w3_low, w3_high = grouped_tile("w3", 0, 2), grouped_tile("w3", 2, 2)
         interleave(on_scalar, w3_low, 0, "w3", 0, 1)
@@ -161,28 +175,44 @@ def tile_picked_ngramgate_none_p_kernel(tc, x_words, x_scales, w1, w2, w3, offs,
         x_own = (own_words[:], x_plane[:, S : 2 * S])
         for b in range(N // P):
             multiply(("w3", b))
-        w1_low, w1_high = grouped_tile("w1", 0, 2), grouped_tile("w1", 2, 2)
+        w1_low = grouped_tile("w1", 0, 2)
+        w1_high = [grouped_tile("w1", b, 1) for b in (2, 3)]
         w2_grouped = [grouped_tile("w2", b, 1) for b in range(N // P)]
         interleave(on_vector, w1_low, 0, "w1", 0, 2)
-        interleave(on_scalar, w1_high, 0, "w1", 2, 1)
-        interleave(on_scalar, w1_high, 1, "w1", 3, 1)
+        for b in (2, 3):
+            interleave(on_scalar, w1_high[b - 2], 0, "w1", b, 1)
+        quantise(w1_high[0], "w1", 2)
         quantise(w1_low, "w1", 0)
-        make_gates([0], "w1_0_raw")
+        make_gates([0], "w1_0_raw", 1)
         interleave(on_vector, w2_grouped[0], 0, "w2", 0, 1)
         interleave(on_scalar, w2_grouped[1], 0, "w2", 1, 1)
-        quantise(w1_high, "w1", 2)
+        quantise(w1_high[1], "w1", 3)
         quantise(w2_grouped[0], "w2", 0)
-        make_gates([1], "w2_0_raw")
+        make_gates([1], "w2_0_raw", 1)
         interleave(on_vector, w2_grouped[2], 0, "w2", 2, 1)
         interleave(on_scalar, w2_grouped[3], 0, "w2", 3, 1)
         quantise(w2_grouped[1], "w2", 1)
         quantise(w2_grouped[2], "w2", 2)
-        for key in (("w1", 0), ("w1", 1), ("w2", 0), ("w1", 2), ("w2", 1), ("w1", 3), ("w2", 2)):
-            multiply(key)
-        finish(0, "w2_2_grouped", 2)
+        two_banks(0)
+        whole_bank(1, "sum_ps1")
+        whole_bank(2, "sum_ps2")
+        whole_bank(3, "gate_ps0")
+        multiply(("w1", 2))
+        multiply(("w1", 0), 0)
+        multiply(("w1", 0), 1)
+        multiply(("w1", 1))
+        multiply(("w2", 0), 0)
+        multiply(("w2", 0), 1)
+        multiply(("w2", 1))
+        multiply(("w2", 2))
+        multiply(("w1", 3))
+        finish(0, 0, "w2_2_grouped")
+        finish(0, 1)
         quantise(w2_grouped[3], "w2", 3)
         multiply(("w2", 3))
         make_gates([2, 3], "w2_3_raw", 2)
-        finish(1, "w2_3_grouped", 2)
-        finish(2, "result2", 2)
-        finish(3, "result3", 2)
+        finish(1, 0, "w2_3_grouped")
+        finish(1, 1, "w2_1_grouped")
+        for b in (2, 3):
+            for half in (0, 1):
+                finish(b, half)

@@ -57,20 +57,13 @@ def tile_picked_ngramgate_none_p_kernel(tc, x_words, x_scales, w1, w2, w3, offs,
             source = x_words[0, :, c0:c1, :].rearrange("p c r -> p (c r)").bitcast(I32)
             nc.sync.dma_start(out=word_table[:, c0:c1].bitcast(I32), in_=source)
 
-        w1_tile = keep.tile([P, PACK, N], F32, name="w1_0_raw", tag="w1_0_raw", align_bytes=64)
-        for b in range(N // P):
-            raw["w1", b] = (w1_tile, b * P)
-
-        def load_w1_rows(j0, j1):
-            nc.sync.dma_start(out=w1_tile[:, j0:j1, :], in_=w1.rearrange("(p j) n -> p j n", j=PACK)[:, j0:j1, :])
-
         load_words(0, 512)
         nc.sync.dma_start(offs_sb[:], offs)
         nc.sync.dma_start(own_sb[:], own)
         load_scales(nc.sync)
         load("w3", 0, 4, nc.sync)
         load_words(512, T)
-        load_w1_rows(0, 2)
+        load("w1", 0, 2, nc.sync)
 
         warm_in = keep.tile([P, 1], F32, name="warm_in")
         warm_out = keep.tile([P, 1], F32, name="warm_out")
@@ -85,18 +78,18 @@ def tile_picked_ngramgate_none_p_kernel(tc, x_words, x_scales, w1, w2, w3, offs,
                 out=x_plane[i:P:QUADRANT, :].bitcast(I32),
                 in_=picked_bytes[BLOCK_PARTITIONS * i : P : QUADRANT, :].bitcast(I32),
             )
-        load_w1_rows(2, 4)
         load("w2", 0, 2, nc.sync)
+        load("w1", 2, 2, nc.sync)
         load("w2", 2, 1, nc.sync)
         load("w2", 3, 1, nc.sync)
 
-        gate_ps = [psum.tile([P, S], F32, name="gate_ps%d" % b, tag="gate_ps%d" % b) for b in range(N // P)]
         sums = {}
         banks = {}
         results = {}
         on_scalar, on_vector = nc.scalar.copy, nc.vector.tensor_copy
         quantised = {}
         gates = {}
+        gate_ps = {}
 
         def grouped_tile(name, first, count):
             label = "%s_%d_grouped" % (name, first)
@@ -108,22 +101,24 @@ def tile_picked_ngramgate_none_p_kernel(tc, x_words, x_scales, w1, w2, w3, offs,
             target = grouped[:, place * P : (place + count) * P, :]
             copy(target.rearrange("p (c i) t -> p c t i", i=LINE), source.rearrange("p t (c i) -> p c t i", i=LINE))
 
-        def quantise(grouped, name, first):
+        def quantise(grouped, name, first, tag=None):
             count = grouped.shape[1] // P
             label = "%s_%d" % (name, first)
-            words = keep.tile([P, count * P], U32, name=label + "_words", align_bytes=64)
+            words = keep.tile([P, count * P], U32, name=label + "_words", tag=tag or label + "_words", align_bytes=64)
             plane = keep.tile([P, count * P], U8, name=label + "_plane", align_bytes=64)
             nc.vector.quantize_mx(out=words[:].bitcast(FP8X4), scales=plane[:], in_=grouped[:].rearrange("p n t -> p (n t)"))
             for b in range(count):
                 quantised[name, first + b] = (words[:, b * P : (b + 1) * P], plane[:, b * P : (b + 1) * P])
 
-        def multiply(key, half=None):
-            name, b = key
-            words, plane = quantised[key]
+        def half_columns(half):
+            return slice(0, S) if half is None else slice(half * S // 2, (half + 1) * S // 2)
+
+        def multiply(name, b, half, target):
+            words, plane = quantised[name, b]
             moving = x_own if name == "w2" else x_hashed
-            columns = slice(0, S) if half is None else slice(half * S // 2, (half + 1) * S // 2)
+            columns = half_columns(half)
             nc.tensor.matmul_mx(
-                out=gate_ps[b][:] if name == "w3" else banks[b, half],
+                out=target,
                 lhsT=words.bitcast(FP8X4),
                 lhsT_scale=plane,
                 rhs=moving[0][:, columns].bitcast(FP8X4),
@@ -132,34 +127,44 @@ def tile_picked_ngramgate_none_p_kernel(tc, x_words, x_scales, w1, w2, w3, offs,
                 stop=name != "w1",
             )
 
+        def add(name, b):
+            for half, target in banks[b]:
+                multiply(name, b, half, target)
+
         def whole_bank(b, tag):
             bank = psum.tile([P, S], F32, name="sum_ps%d" % b, tag=tag)
-            banks[b, None] = bank[:]
+            banks[b] = [(None, bank[:])]
             for half in (0, 1):
-                sums[b, half] = bank[:, half * S // 2 : (half + 1) * S // 2]
+                sums[b, half] = bank[:, half_columns(half)]
 
-        def two_banks(b):
+        def two_banks(b, tags):
+            banks[b] = []
             for half in (0, 1):
-                bank = psum.tile([P, S], F32, name="sum_ps%d_%d" % (b, half))
-                banks[b, half] = bank[:, 0 : S // 2]
+                bank = psum.tile([P, S], F32, name="sum_ps%d_%d" % (b, half), tag=tags[half])
+                banks[b].append((half, bank[:, 0 : S // 2]))
                 sums[b, half] = bank[:, 0 : S // 2]
 
-        def make_gates(blocks, tag, pieces):
-            tile = keep.tile([P, len(blocks), S], F32, name="gate%d" % blocks[0], tag=tag, align_bytes=64)
-            for place, b in enumerate(blocks):
-                gates[b] = tile[:, place, :]
-                count = pieces if b == blocks[-1] else 1
-                for piece in range(count):
-                    columns = slice(piece * S // count, (piece + 1) * S // count)
-                    nc.scalar.activation(gates[b][:, columns], gate_ps[b][:, columns], SIGMOID)
+        def gate_pass(b, tag=None):
+            gate_ps[b] = psum.tile([P, S], F32, name="gate_ps%d" % b, tag=tag or "gate_ps%d" % b)
+            multiply("w3", b, None, gate_ps[b][:])
 
-        def finish(b, half, tag=None):
-            name = "result%d_%d" % (b, half)
-            columns = slice(half * S // 2, (half + 1) * S // 2)
-            result = keep.tile([P, S // 2], F32, name=name, tag=tag or name, align_bytes=64)
+        def behind(tag, pieces):
+            return keep.tile([P, pieces, S // 2], F32, name="behind_" + tag, tag=tag, align_bytes=64)
+
+        def make_gate(b, tile, place, pieces=1):
+            target = tile[:, place : place + 2, :].rearrange("p h c -> p (h c)")
+            for piece in range(pieces):
+                columns = slice(piece * S // pieces, (piece + 1) * S // pieces)
+                nc.scalar.activation(target[:, columns], gate_ps[b][:, columns], SIGMOID)
+            for half in (0, 1):
+                gates[b, half] = tile[:, place + half, :]
+
+        def finish(b, half, result=None):
+            if result is None:
+                result = keep.tile([P, S // 2], F32, name="result%d_%d" % (b, half), align_bytes=64)[:]
             results[b, half] = result
-            nc.vector.tensor_tensor(result[:], sums[b, half], gates[b][:, columns], MULT)
-            nc.sync.dma_start(out=out[b * P : (b + 1) * P, columns], in_=result[:])
+            nc.vector.tensor_tensor(result, sums[b, half], gates[b, half], MULT)
+            nc.sync.dma_start(out=out[b * P : (b + 1) * P, half_columns(half)], in_=result)
 
         w3_low, w3_high = grouped_tile("w3", 0, 2), grouped_tile("w3", 2, 2)
         interleave(on_scalar, w3_low, 0, "w3", 0, 1)
@@ -173,46 +178,47 @@ def tile_picked_ngramgate_none_p_kernel(tc, x_words, x_scales, w1, w2, w3, offs,
         nc.vector.tensor_copy(own_words[:], word_table[:].indirect(own_sb[:]))
         x_hashed = (hashed_words[:], x_plane[:, 0:S])
         x_own = (own_words[:], x_plane[:, S : 2 * S])
-        for b in range(N // P):
-            multiply(("w3", b))
-        w1_low = grouped_tile("w1", 0, 2)
-        w1_high = [grouped_tile("w1", b, 1) for b in (2, 3)]
+        for b in (0, 1, 2):
+            gate_pass(b)
+        w1_low, w1_high = grouped_tile("w1", 0, 2), grouped_tile("w1", 2, 2)
         w2_grouped = [grouped_tile("w2", b, 1) for b in range(N // P)]
-        interleave(on_vector, w1_low, 0, "w1", 0, 2)
-        for b in (2, 3):
-            interleave(on_scalar, w1_high[b - 2], 0, "w1", b, 1)
-        quantise(w1_high[0], "w1", 2)
+        interleave(on_scalar, w1_low, 0, "w1", 0, 2)
+        early = behind("w1_0_raw", 4)
+        make_gate(0, early, 0)
+        make_gate(1, early, 2)
         quantise(w1_low, "w1", 0)
-        make_gates([0], "w1_0_raw", 1)
-        interleave(on_vector, w2_grouped[0], 0, "w2", 0, 1)
-        interleave(on_scalar, w2_grouped[1], 0, "w2", 1, 1)
-        quantise(w1_high[1], "w1", 3)
-        quantise(w2_grouped[0], "w2", 0)
-        make_gates([1], "w2_0_raw", 1)
-        interleave(on_vector, w2_grouped[2], 0, "w2", 2, 1)
-        interleave(on_scalar, w2_grouped[3], 0, "w2", 3, 1)
-        quantise(w2_grouped[1], "w2", 1)
+        for b in (0, 1):
+            interleave(on_vector, w2_grouped[b], 0, "w2", b, 1)
+        for b in (0, 1):
+            quantise(w2_grouped[b], "w2", b)
+        interleave(on_vector, w1_high, 0, "w1", 2, 1)
+        interleave(on_scalar, w1_high, 1, "w1", 3, 1)
+        for b in (2, 3):
+            interleave(on_scalar, w2_grouped[b], 0, "w2", b, 1)
+        two_banks(0, ("sum0_0", "sum0_1"))
+        whole_bank(1, "sum1")
+        whole_bank(2, "sum2")
+        two_banks(3, ("gate_ps0", "gate_ps1"))
+        add("w1", 0)
+        add("w2", 0)
+        add("w1", 1)
+        add("w2", 1)
+        first_results = behind("w1_2_raw", 2)
+        finish(0, 0, first_results[:, 0, :])
+        gate_pass(3, "sum0_0")
+        quantise(w1_high, "w1", 2)
+        add("w1", 2)
+        finish(0, 1, first_results[:, 1, :])
         quantise(w2_grouped[2], "w2", 2)
-        two_banks(0)
-        whole_bank(1, "sum_ps1")
-        whole_bank(2, "sum_ps2")
-        whole_bank(3, "gate_ps0")
-        multiply(("w1", 2))
-        multiply(("w1", 0), 0)
-        multiply(("w1", 0), 1)
-        multiply(("w1", 1))
-        multiply(("w2", 0), 0)
-        multiply(("w2", 0), 1)
-        multiply(("w2", 1))
-        multiply(("w2", 2))
-        multiply(("w1", 3))
-        finish(0, 0, "w2_2_grouped")
-        finish(0, 1)
+        add("w2", 2)
+        add("w1", 3)
+        finish(1, 0, behind("w2_2_raw", 1)[:, 0, :])
         quantise(w2_grouped[3], "w2", 3)
-        multiply(("w2", 3))
-        make_gates([2, 3], "w2_3_raw", 2)
-        finish(1, 0, "w2_3_grouped")
-        finish(1, 1, "w2_1_grouped")
+        add("w2", 3)
+        late = behind("w2_3_raw", 5)
+        make_gate(2, late, 1, 2)
+        make_gate(3, late, 3, 2)
+        finish(1, 1, late[:, 0, :])
         for b in (2, 3):
             for half in (0, 1):
                 finish(b, half)

@@ -88,6 +88,7 @@ def tile_picked_ngramgate_none_p_kernel(tc, x_words, x_scales, w1, w2, w3, offs,
         results = {}
         on_scalar, on_vector = nc.scalar.copy, nc.vector.tensor_copy
         quantised = {}
+        codes = {}
         gates = {}
         gate_ps = {}
 
@@ -107,6 +108,7 @@ def tile_picked_ngramgate_none_p_kernel(tc, x_words, x_scales, w1, w2, w3, offs,
             words = keep.tile([P, count * P], U32, name=label + "_words", tag=tag or label + "_words", align_bytes=64)
             plane = keep.tile([P, count * P], U8, name=label + "_plane", align_bytes=64)
             nc.vector.quantize_mx(out=words[:].bitcast(FP8X4), scales=plane[:], in_=grouped[:].rearrange("p n t -> p (n t)"))
+            codes[name, first] = (words[:], plane[:])
             for b in range(count):
                 quantised[name, first + b] = (words[:, b * P : (b + 1) * P], plane[:, b * P : (b + 1) * P])
 
@@ -172,6 +174,18 @@ def tile_picked_ngramgate_none_p_kernel(tc, x_words, x_scales, w1, w2, w3, offs,
         interleave(on_vector, w3_high, 0, "w3", 2, 2)
         quantise(w3_low, "w3", 0)
         quantise(w3_high, "w3", 2)
+        warm_ps = psum.tile([P, S], F32, name="warm_ps", tag="sum2")
+        warm_words, warm_plane = quantised["w3", 3]
+        for half in (0, 1):
+            nc.tensor.matmul_mx(
+                out=warm_ps[:, half_columns(half)],
+                lhsT=warm_words.bitcast(FP8X4),
+                lhsT_scale=warm_plane,
+                rhs=codes["w3", 2][0].bitcast(FP8X4),
+                rhs_scale=codes["w3", 2][1],
+                start=True,
+                stop=True,
+            )
         hashed_words = keep.tile([P, S], U32, name="hashed_words", align_bytes=64)
         own_words = keep.tile([P, S], U32, name="own_words", align_bytes=64)
         nc.vector.tensor_copy(hashed_words[:], word_table[:].indirect(offs_sb[:]))

@@ -21,8 +21,9 @@ GROUP = 16
 BLOCK_PARTITIONS = 8
 QUADRANT = 32
 PLANE_ROWS = QUADRANT // BLOCK_PARTITIONS
-HALF = N // 2
+HALF = S // 2
 LINE = 2
+FIRST_WORDS = 512
 
 
 def tile_picked_ngramgate_none_p_kernel(tc, x_words, x_scales, w1, w2, w3, offs, own, out):
@@ -34,11 +35,11 @@ def tile_picked_ngramgate_none_p_kernel(tc, x_words, x_scales, w1, w2, w3, offs,
         weights = {"w1": w1, "w2": w2, "w3": w3}
         raw = {}
 
-        def load(name, first, count, queue):
+        def load_parts(name, first, count):
             tag = "%s_%d_raw" % (name, first)
             tile = keep.tile([P, PACK, count * P], F32, name=tag, tag=tag, align_bytes=64)
             columns = weights[name][:, first * P : (first + count) * P]
-            queue.dma_start(out=tile[:], in_=columns.rearrange("(p j) n -> p j n", j=PACK))
+            nc.sync.dma_start(out=tile[:], in_=columns.rearrange("(p j) n -> p j n", j=PACK))
             for b in range(count):
                 raw[name, first + b] = (tile, b * P)
 
@@ -50,20 +51,17 @@ def tile_picked_ngramgate_none_p_kernel(tc, x_words, x_scales, w1, w2, w3, offs,
         nc.vector.memset(x_plane[:].bitcast(I32), 0)
         word_table = keep.tile([P, T], U32, name="word_table", align_bytes=64)
 
-        def load_scales(queue):
-            queue.dma_start(out=byte_table[0:P:BLOCK_PARTITIONS, :].bitcast(I32), in_=x_scales[0].bitcast(I32))
-
         def load_words(c0, c1):
             source = x_words[0, :, c0:c1, :].rearrange("p c r -> p (c r)").bitcast(I32)
             nc.sync.dma_start(out=word_table[:, c0:c1].bitcast(I32), in_=source)
 
-        load_words(0, 512)
+        load_words(0, FIRST_WORDS)
         nc.sync.dma_start(offs_sb[:], offs)
         nc.sync.dma_start(own_sb[:], own)
-        load_scales(nc.sync)
-        load("w3", 0, 4, nc.sync)
-        load_words(512, T)
-        load("w1", 0, 2, nc.sync)
+        nc.sync.dma_start(out=byte_table[0:P:BLOCK_PARTITIONS, :].bitcast(I32), in_=x_scales[0].bitcast(I32))
+        load_parts("w3", 0, 4)
+        load_words(FIRST_WORDS, T)
+        load_parts("w1", 0, 2)
 
         warm_in = keep.tile([P, 1], F32, name="warm_in")
         warm_out = keep.tile([P, 1], F32, name="warm_out")
@@ -78,19 +76,18 @@ def tile_picked_ngramgate_none_p_kernel(tc, x_words, x_scales, w1, w2, w3, offs,
                 out=x_plane[i:P:QUADRANT, :].bitcast(I32),
                 in_=picked_bytes[BLOCK_PARTITIONS * i : P : QUADRANT, :].bitcast(I32),
             )
-        load("w2", 0, 2, nc.sync)
-        load("w1", 2, 2, nc.sync)
-        load("w2", 2, 1, nc.sync)
-        load("w2", 3, 1, nc.sync)
 
-        sums = {}
-        banks = {}
-        results = {}
+        load_parts("w2", 0, 2)
+        load_parts("w1", 2, 2)
+        load_parts("w2", 2, 1)
+        load_parts("w2", 3, 1)
+
         on_scalar, on_vector = nc.scalar.copy, nc.vector.tensor_copy
         quantised = {}
-        codes = {}
-        gates = {}
+        banks = {}
+        sums = {}
         gate_ps = {}
+        gates = {}
 
         def grouped_tile(name, first, count):
             label = "%s_%d_grouped" % (name, first)
@@ -102,29 +99,29 @@ def tile_picked_ngramgate_none_p_kernel(tc, x_words, x_scales, w1, w2, w3, offs,
             target = grouped[:, place * P : (place + count) * P, :]
             copy(target.rearrange("p (c i) t -> p c t i", i=LINE), source.rearrange("p t (c i) -> p c t i", i=LINE))
 
-        def quantise(grouped, name, first, tag=None):
+        def quantise(grouped, name, first):
             count = grouped.shape[1] // P
             label = "%s_%d" % (name, first)
-            words = keep.tile([P, count * P], U32, name=label + "_words", tag=tag or label + "_words", align_bytes=64)
+            words = keep.tile([P, count * P], U32, name=label + "_words", tag=label + "_words", align_bytes=64)
             plane = keep.tile([P, count * P], U8, name=label + "_plane", align_bytes=64)
             nc.vector.quantize_mx(out=words[:].bitcast(FP8X4), scales=plane[:], in_=grouped[:].rearrange("p n t -> p (n t)"))
-            codes[name, first] = (words[:], plane[:])
             for b in range(count):
                 quantised[name, first + b] = (words[:, b * P : (b + 1) * P], plane[:, b * P : (b + 1) * P])
+            return words[:], plane[:]
 
         def half_columns(half):
-            return slice(0, S) if half is None else slice(half * S // 2, (half + 1) * S // 2)
+            return slice(0, S) if half is None else slice(half * HALF, (half + 1) * HALF)
 
         def multiply(name, b, half, target):
             words, plane = quantised[name, b]
-            moving = x_own if name == "w2" else x_hashed
+            moving_words, moving_plane = x_own if name == "w2" else x_hashed
             columns = half_columns(half)
             nc.tensor.matmul_mx(
                 out=target,
                 lhsT=words.bitcast(FP8X4),
                 lhsT_scale=plane,
-                rhs=moving[0][:, columns].bitcast(FP8X4),
-                rhs_scale=moving[1][:, columns],
+                rhs=moving_words[:, columns].bitcast(FP8X4),
+                rhs_scale=moving_plane[:, columns],
                 start=name != "w2",
                 stop=name != "w1",
             )
@@ -143,17 +140,17 @@ def tile_picked_ngramgate_none_p_kernel(tc, x_words, x_scales, w1, w2, w3, offs,
             banks[b] = []
             for half in (0, 1):
                 bank = psum.tile([P, S], F32, name="sum_ps%d_%d" % (b, half), tag=tags[half])
-                banks[b].append((half, bank[:, 0 : S // 2]))
-                sums[b, half] = bank[:, 0 : S // 2]
+                banks[b].append((half, bank[:, 0:HALF]))
+                sums[b, half] = bank[:, 0:HALF]
 
-        def gate_pass(b, tag=None):
-            gate_ps[b] = psum.tile([P, S], F32, name="gate_ps%d" % b, tag=tag or "gate_ps%d" % b)
+        def gate_pass(b, tag):
+            gate_ps[b] = psum.tile([P, S], F32, name="gate_ps%d" % b, tag=tag)
             multiply("w3", b, None, gate_ps[b][:])
 
-        def behind(tag, pieces):
-            return keep.tile([P, pieces, S // 2], F32, name="behind_" + tag, tag=tag, align_bytes=64)
+        def behind(tag, halves):
+            return keep.tile([P, halves, HALF], F32, name="behind_" + tag, tag=tag, align_bytes=64)
 
-        def make_gate(b, tile, place, pieces=1):
+        def make_gate(b, tile, place, pieces):
             target = tile[:, place : place + 2, :].rearrange("p h c -> p (h c)")
             for piece in range(pieces):
                 columns = slice(piece * S // pieces, (piece + 1) * S // pieces)
@@ -161,10 +158,7 @@ def tile_picked_ngramgate_none_p_kernel(tc, x_words, x_scales, w1, w2, w3, offs,
             for half in (0, 1):
                 gates[b, half] = tile[:, place + half, :]
 
-        def finish(b, half, result=None):
-            if result is None:
-                result = keep.tile([P, S // 2], F32, name="result%d_%d" % (b, half), align_bytes=64)[:]
-            results[b, half] = result
+        def finish(b, half, result):
             nc.vector.tensor_tensor(result, sums[b, half], gates[b, half], MULT)
             nc.sync.dma_start(out=out[b * P : (b + 1) * P, half_columns(half)], in_=result)
 
@@ -173,7 +167,8 @@ def tile_picked_ngramgate_none_p_kernel(tc, x_words, x_scales, w1, w2, w3, offs,
         interleave(on_vector, w3_low, 1, "w3", 1, 1)
         interleave(on_vector, w3_high, 0, "w3", 2, 2)
         quantise(w3_low, "w3", 0)
-        quantise(w3_high, "w3", 2)
+        high_words, high_plane = quantise(w3_high, "w3", 2)
+
         warm_ps = psum.tile([P, S], F32, name="warm_ps", tag="sum2")
         warm_words, warm_plane = quantised["w3", 3]
         for half in (0, 1):
@@ -181,11 +176,12 @@ def tile_picked_ngramgate_none_p_kernel(tc, x_words, x_scales, w1, w2, w3, offs,
                 out=warm_ps[:, half_columns(half)],
                 lhsT=warm_words.bitcast(FP8X4),
                 lhsT_scale=warm_plane,
-                rhs=codes["w3", 2][0].bitcast(FP8X4),
-                rhs_scale=codes["w3", 2][1],
+                rhs=high_words.bitcast(FP8X4),
+                rhs_scale=high_plane,
                 start=True,
                 stop=True,
             )
+
         hashed_words = keep.tile([P, S], U32, name="hashed_words", align_bytes=64)
         own_words = keep.tile([P, S], U32, name="own_words", align_bytes=64)
         nc.vector.tensor_copy(hashed_words[:], word_table[:].indirect(offs_sb[:]))
@@ -193,22 +189,25 @@ def tile_picked_ngramgate_none_p_kernel(tc, x_words, x_scales, w1, w2, w3, offs,
         x_hashed = (hashed_words[:], x_plane[:, 0:S])
         x_own = (own_words[:], x_plane[:, S : 2 * S])
         for b in (0, 1, 2):
-            gate_pass(b)
-        w1_low, w1_high = grouped_tile("w1", 0, 2), grouped_tile("w1", 2, 2)
+            gate_pass(b, "gate_ps%d" % b)
+
+        w1_low, w1_third, w1_last = grouped_tile("w1", 0, 2), grouped_tile("w1", 2, 1), grouped_tile("w1", 3, 1)
         w2_grouped = [grouped_tile("w2", b, 1) for b in range(N // P)]
         interleave(on_scalar, w1_low, 0, "w1", 0, 2)
-        early = behind("w1_0_raw", 4)
-        make_gate(0, early, 0)
-        make_gate(1, early, 2)
+        early_gates = behind("w1_0_raw", 4)
+        make_gate(0, early_gates, 0, 1)
+        make_gate(1, early_gates, 2, 1)
         quantise(w1_low, "w1", 0)
         for b in (0, 1):
             interleave(on_vector, w2_grouped[b], 0, "w2", b, 1)
         for b in (0, 1):
             quantise(w2_grouped[b], "w2", b)
-        interleave(on_vector, w1_high, 0, "w1", 2, 1)
-        interleave(on_scalar, w1_high, 1, "w1", 3, 1)
+
+        interleave(on_vector, w1_third, 0, "w1", 2, 1)
+        interleave(on_scalar, w1_last, 0, "w1", 3, 1)
         for b in (2, 3):
             interleave(on_scalar, w2_grouped[b], 0, "w2", b, 1)
+
         two_banks(0, ("sum0_0", "sum0_1"))
         whole_bank(1, "sum1")
         whole_bank(2, "sum2")
@@ -217,11 +216,13 @@ def tile_picked_ngramgate_none_p_kernel(tc, x_words, x_scales, w1, w2, w3, offs,
         add("w2", 0)
         add("w1", 1)
         add("w2", 1)
+
+        quantise(w1_third, "w1", 2)
+        add("w1", 2)
         first_results = behind("w1_2_raw", 2)
         finish(0, 0, first_results[:, 0, :])
         gate_pass(3, "sum0_0")
-        quantise(w1_high, "w1", 2)
-        add("w1", 2)
+        quantise(w1_last, "w1", 3)
         finish(0, 1, first_results[:, 1, :])
         quantise(w2_grouped[2], "w2", 2)
         add("w2", 2)
@@ -229,10 +230,12 @@ def tile_picked_ngramgate_none_p_kernel(tc, x_words, x_scales, w1, w2, w3, offs,
         finish(1, 0, behind("w2_2_raw", 1)[:, 0, :])
         quantise(w2_grouped[3], "w2", 3)
         add("w2", 3)
+
         late = behind("w2_3_raw", 5)
         make_gate(2, late, 1, 2)
         make_gate(3, late, 3, 2)
         finish(1, 1, late[:, 0, :])
         for b in (2, 3):
             for half in (0, 1):
-                finish(b, half)
+                result = keep.tile([P, HALF], F32, name="result%d_%d" % (b, half), align_bytes=64)
+                finish(b, half, result[:])

@@ -14,6 +14,7 @@ U8 = mybir.dt.uint8
 FP8X4 = mybir.dt.float8_e4m3fn_x4
 SIGMOID = mybir.ActivationFunctionType.Sigmoid
 MULT = mybir.AluOpType.mult
+ADD = mybir.AluOpType.add
 
 P = 128
 PACK = 4
@@ -98,6 +99,11 @@ def tile_picked_ngramgate_none_p_kernel(tc, x_words, x_scales, w1, w2, w3, offs,
             source = tile[:, :, c0 : c0 + count * P]
             target = grouped[:, place * P : (place + count) * P, :]
             copy(target.rearrange("p (c i) t -> p c t i", i=LINE), source.rearrange("p t (c i) -> p c t i", i=LINE))
+
+        def interleave_on_gpsimd(grouped, place, name, first):
+            tile, c0 = raw[name, first]
+            source = tile[:, :, c0 : c0 + P].rearrange("p t c -> p c t")
+            nc.gpsimd.tensor_scalar(grouped[:, place * P : (place + 1) * P, :], source, 1.0, 0.0, MULT, ADD)
 
         def quantise(grouped, name, first):
             count = grouped.shape[1] // P
@@ -193,7 +199,8 @@ def tile_picked_ngramgate_none_p_kernel(tc, x_words, x_scales, w1, w2, w3, offs,
 
         w1_low, w1_third, w1_last = grouped_tile("w1", 0, 2), grouped_tile("w1", 2, 1), grouped_tile("w1", 3, 1)
         w2_grouped = [grouped_tile("w2", b, 1) for b in range(N // P)]
-        interleave(on_scalar, w1_low, 0, "w1", 0, 2)
+        interleave(on_scalar, w1_low, 0, "w1", 0, 1)
+        interleave_on_gpsimd(w1_low, 1, "w1", 1)
         early_gates = behind("w1_0_raw", 4)
         make_gate(0, early_gates, 0, 1)
         make_gate(1, early_gates, 2, 1)

@@ -94,10 +94,11 @@ def tile_picked_ngramgate_none_p_kernel(tc, x_words, x_scales, w1, w2, w3, offs,
             label = "%s_%d_grouped" % (name, first)
             return keep.tile([P, count * P, PACK], BF16, name=label, tag=label, align_bytes=64)
 
-        def interleave(copy, grouped, place, name, first, count):
+        def interleave(copy, grouped, place, name, first, count, skip=0, width=None):
             tile, c0 = raw[name, first]
-            source = tile[:, :, c0 : c0 + count * P]
-            target = grouped[:, place * P : (place + count) * P, :]
+            width = width or count * P
+            source = tile[:, :, c0 + skip : c0 + skip + width]
+            target = grouped[:, place * P + skip : place * P + skip + width, :]
             copy(target.rearrange("p (c i) t -> p c t i", i=LINE), source.rearrange("p t (c i) -> p c t i", i=LINE))
 
         def interleave_on_gpsimd(grouped, place, name, first):
@@ -171,7 +172,8 @@ def tile_picked_ngramgate_none_p_kernel(tc, x_words, x_scales, w1, w2, w3, offs,
         w3_low, w3_high = grouped_tile("w3", 0, 2), grouped_tile("w3", 2, 2)
         interleave(on_scalar, w3_low, 0, "w3", 0, 1)
         interleave(on_vector, w3_low, 1, "w3", 1, 1)
-        interleave(on_vector, w3_high, 0, "w3", 2, 2)
+        interleave(on_vector, w3_high, 0, "w3", 2, 2, 0, 3 * P // 2)
+        interleave(on_scalar, w3_high, 0, "w3", 2, 2, 3 * P // 2, P // 2)
         quantise(w3_low, "w3", 0)
         high_words, high_plane = quantise(w3_high, "w3", 2)
 
@@ -234,14 +236,14 @@ def tile_picked_ngramgate_none_p_kernel(tc, x_words, x_scales, w1, w2, w3, offs,
         quantise(w2_grouped[2], "w2", 2)
         add("w2", 2)
         add("w1", 3)
-        finish(1, 0, behind("w2_2_raw", 1)[:, 0, :])
+        late = behind("w2_2_raw", 5)
+        finish(1, 0, late[:, 0, :])
         quantise(w2_grouped[3], "w2", 3)
         add("w2", 3)
 
-        late = behind("w2_3_raw", 5)
         make_gate(2, late, 1, 2)
         make_gate(3, late, 3, 2)
-        finish(1, 1, late[:, 0, :])
+        finish(1, 1, behind("w2_3_raw", 1)[:, 0, :])
         for b in (2, 3):
             for half in (0, 1):
                 result = keep.tile([P, HALF], F32, name="result%d_%d" % (b, half), align_bytes=64)

@@ -34,13 +34,16 @@ def tile_picked_ngramgate_none_p_kernel(tc, x_words, x_scales, w1, w2, w3, offs,
         psum = ctx.enter_context(tc.psum_pool(name="psum", bufs=1))
 
         weights = {"w1": w1, "w2": w2, "w3": w3}
+        spaces = {}
         raw = {}
 
-        def load_parts(name, first, count):
+        def load_parts(name, first, count, room=0):
             tag = "%s_%d_raw" % (name, first)
-            tile = keep.tile([P, PACK, count * P], F32, name=tag, tag=tag, align_bytes=64)
+            space = keep.tile([P, PACK * (room + count * P)], F32, name=tag, tag=tag, align_bytes=64)
+            spaces[name, first] = space
+            tile = space[:].rearrange("p (j n) -> p j n", j=PACK)[:, :, room:]
             columns = weights[name][:, first * P : (first + count) * P]
-            nc.sync.dma_start(out=tile[:], in_=columns.rearrange("(p j) n -> p j n", j=PACK))
+            nc.sync.dma_start(out=tile, in_=columns.rearrange("(p j) n -> p j n", j=PACK))
             for b in range(count):
                 raw[name, first + b] = (tile, b * P)
 
@@ -79,7 +82,7 @@ def tile_picked_ngramgate_none_p_kernel(tc, x_words, x_scales, w1, w2, w3, offs,
             )
 
         load_parts("w2", 0, 2)
-        load_parts("w1", 2, 2)
+        load_parts("w1", 2, 2, HALF - P // 2)
         load_parts("w2", 2, 1)
         load_parts("w2", 3, 1)
 
@@ -106,20 +109,20 @@ def tile_picked_ngramgate_none_p_kernel(tc, x_words, x_scales, w1, w2, w3, offs,
             source = tile[:, :, c0 : c0 + P].rearrange("p t c -> p c t")
             nc.gpsimd.tensor_scalar(grouped[:, place * P : (place + 1) * P, :], source, 1.0, 0.0, MULT, ADD)
 
-        def quantise(grouped, name, first):
+        def quantise(grouped, name, first, parts=None):
             count = grouped.shape[1] // P
             label = "%s_%d" % (name, first)
             words = keep.tile([P, count * P], U32, name=label + "_words", tag=label + "_words", align_bytes=64)
             plane = keep.tile([P, count * P], U8, name=label + "_plane", align_bytes=64)
             nc.vector.quantize_mx(out=words[:].bitcast(FP8X4), scales=plane[:], in_=grouped[:].rearrange("p n t -> p (n t)"))
             for b in range(count):
-                quantised[name, first + b] = (words[:, b * P : (b + 1) * P], plane[:, b * P : (b + 1) * P])
+                quantised[parts[b] if parts else (name, first + b)] = (words[:, b * P : (b + 1) * P], plane[:, b * P : (b + 1) * P])
             return words[:], plane[:]
 
         def half_columns(half):
             return slice(0, S) if half is None else slice(half * HALF, (half + 1) * HALF)
 
-        def multiply(name, b, half, target):
+        def multiply(name, b, half, target, opener="w1"):
             words, plane = quantised[name, b]
             moving_words, moving_plane = x_own if name == "w2" else x_hashed
             columns = half_columns(half)
@@ -129,8 +132,8 @@ def tile_picked_ngramgate_none_p_kernel(tc, x_words, x_scales, w1, w2, w3, offs,
                 lhsT_scale=plane,
                 rhs=moving_words[:, columns].bitcast(FP8X4),
                 rhs_scale=moving_plane[:, columns],
-                start=name != "w2",
-                stop=name != "w1",
+                start=name in ("w3", opener),
+                stop=name != opener,
             )
 
         def add(name, b):
@@ -164,6 +167,10 @@ def tile_picked_ngramgate_none_p_kernel(tc, x_words, x_scales, w1, w2, w3, offs,
                 nc.scalar.activation(target[:, columns], gate_ps[b][:, columns], SIGMOID)
             for half in (0, 1):
                 gates[b, half] = tile[:, place + half, :]
+
+        def half_gate(b, half, target):
+            nc.scalar.activation(target, gate_ps[b][:, half_columns(half)], SIGMOID)
+            gates[b, half] = target
 
         def finish(b, half, result):
             nc.vector.tensor_tensor(result, sums[b, half], gates[b, half], MULT)
@@ -199,50 +206,54 @@ def tile_picked_ngramgate_none_p_kernel(tc, x_words, x_scales, w1, w2, w3, offs,
         for b in (0, 1, 2):
             gate_pass(b, "gate_ps%d" % b)
 
-        w1_low, w1_third, w1_last = grouped_tile("w1", 0, 2), grouped_tile("w1", 2, 1), grouped_tile("w1", 3, 1)
-        w2_grouped = [grouped_tile("w2", b, 1) for b in range(N // P)]
-        interleave(on_scalar, w1_low, 0, "w1", 0, 1)
-        interleave_on_gpsimd(w1_low, 1, "w1", 1)
-        early_gates = behind("w1_0_raw", 4)
+        w1_first, second = grouped_tile("w1", 0, 1), grouped_tile("second", 1, 2)
+        w1_high = grouped_tile("w1", 2, 2)
+        w2_grouped = {b: grouped_tile("w2", b, 1) for b in (0, 2, 3)}
+        interleave(on_scalar, w1_first, 0, "w1", 0, 1)
+        interleave_on_gpsimd(second, 0, "w1", 1)
+        early_gates = behind("w1_0_raw", 5)
         make_gate(0, early_gates, 0, 1)
         make_gate(1, early_gates, 2, 1)
-        quantise(w1_low, "w1", 0)
-        for b in (0, 1):
-            interleave(on_vector, w2_grouped[b], 0, "w2", b, 1)
-        for b in (0, 1):
-            quantise(w2_grouped[b], "w2", b)
+        half_gate(2, 0, early_gates[:, 4, :])
+        quantise(w1_first, "w1", 0)
+        interleave(on_vector, w2_grouped[0], 0, "w2", 0, 1)
+        interleave(on_vector, second, 1, "w2", 1, 1)
+        quantise(w2_grouped[0], "w2", 0)
+        quantise(second, "second", 1, (("w1", 1), ("w2", 1)))
 
-        interleave(on_vector, w1_third, 0, "w1", 2, 1)
-        interleave(on_scalar, w1_last, 0, "w1", 3, 1)
-        for b in (2, 3):
-            interleave(on_scalar, w2_grouped[b], 0, "w2", b, 1)
+        interleave(on_vector, w1_high, 0, "w1", 2, 2, 0, 64)
+        interleave(on_vector, w1_high, 0, "w1", 2, 2, 64, 96)
+        interleave(on_scalar, w1_high, 0, "w1", 2, 2, 160, 96)
+        interleave(on_scalar, w2_grouped[2], 0, "w2", 2, 1)
+        interleave(on_scalar, w2_grouped[3], 0, "w2", 3, 1, 0, 96)
 
         two_banks(0, ("sum0_0", "sum0_1"))
         whole_bank(1, "sum1")
         whole_bank(2, "sum2")
         two_banks(3, ("gate_ps0", "gate_ps1"))
-        add("w1", 0)
-        add("w2", 0)
+        for (half, target), order in zip(banks[0], (("w1", "w2"), ("w2", "w1"))):
+            for name in order:
+                multiply(name, 0, half, target, order[0])
         add("w1", 1)
         add("w2", 1)
 
-        quantise(w1_third, "w1", 2)
-        add("w1", 2)
-        first_results = behind("w1_2_raw", 2)
-        finish(0, 0, first_results[:, 0, :])
+        pitch = spaces["w1", 2].shape[1] // PACK
+        finish(0, 0, spaces["w1", 2][:, 0:HALF])
         gate_pass(3, "sum0_0")
-        quantise(w1_last, "w1", 3)
-        finish(0, 1, first_results[:, 1, :])
+        finish(0, 1, spaces["w1", 2][:, pitch : pitch + HALF])
+        quantise(w1_high, "w1", 2)
+        add("w1", 2)
+        interleave(on_vector, w2_grouped[3], 0, "w2", 3, 1, 96, 32)
         quantise(w2_grouped[2], "w2", 2)
         add("w2", 2)
         add("w1", 3)
-        late = behind("w2_2_raw", 5)
+        late = behind("w2_2_raw", 4)
         finish(1, 0, late[:, 0, :])
         quantise(w2_grouped[3], "w2", 3)
         add("w2", 3)
 
-        make_gate(2, late, 1, 2)
-        make_gate(3, late, 3, 2)
+        half_gate(2, 1, late[:, 1, :])
+        make_gate(3, late, 2, 2)
         finish(1, 1, behind("w2_3_raw", 1)[:, 0, :])
         for b in (2, 3):
             for half in (0, 1):

@@ -203,7 +203,12 @@ def tile_picked_ngramgate_none_p_kernel(tc, x_words, x_scales, w1, w2, w3, offs,
         nc.vector.tensor_copy(own_words[:], word_table[:].indirect(own_sb[:]))
         x_hashed = (hashed_words[:], x_plane[:, 0:S])
         x_own = (own_words[:], x_plane[:, S : 2 * S])
-        for b in (0, 1, 2):
+        first_ps = []
+        for half, tag in enumerate(("gate_ps0", "gate_ps0_1")):
+            bank = psum.tile([P, S], F32, name="gate_ps0_%d" % half, tag=tag)
+            first_ps.append(bank[:, 0:HALF])
+            multiply("w3", 0, half, first_ps[half])
+        for b in (1, 2):
             gate_pass(b, "gate_ps%d" % b)
 
         w1_first, second = grouped_tile("w1", 0, 1), grouped_tile("second", 1, 2)
@@ -212,7 +217,9 @@ def tile_picked_ngramgate_none_p_kernel(tc, x_words, x_scales, w1, w2, w3, offs,
         interleave(on_scalar, w1_first, 0, "w1", 0, 1)
         interleave_on_gpsimd(second, 0, "w1", 1)
         early_gates = behind("w1_0_raw", 5)
-        make_gate(0, early_gates, 0, 1)
+        for half in (0, 1):
+            nc.scalar.activation(early_gates[:, half, :], first_ps[half], SIGMOID)
+            gates[0, half] = early_gates[:, half, :]
         make_gate(1, early_gates, 2, 1)
         half_gate(2, 0, early_gates[:, 4, :])
         quantise(w1_first, "w1", 0)
@@ -222,8 +229,8 @@ def tile_picked_ngramgate_none_p_kernel(tc, x_words, x_scales, w1, w2, w3, offs,
         quantise(second, "second", 1, (("w1", 1), ("w2", 1)))
 
         interleave(on_vector, w1_high, 0, "w1", 2, 2, 0, 64)
-        interleave(on_vector, w1_high, 0, "w1", 2, 2, 64, 96)
-        interleave(on_scalar, w1_high, 0, "w1", 2, 2, 160, 96)
+        interleave(on_vector, w1_high, 0, "w1", 2, 2, 64, 64)
+        interleave(on_scalar, w1_high, 0, "w1", 2, 2, 128, 128)
         interleave(on_scalar, w2_grouped[2], 0, "w2", 2, 1)
         interleave(on_scalar, w2_grouped[3], 0, "w2", 3, 1, 0, 96)
 

from contextlib import ExitStack

import concourse.mybir as mybir

K, T, S, N = 512, 2048, 512, 512
FLOPS = 3 * 2 * K * N * S

F32 = mybir.dt.float32
BF16 = mybir.dt.bfloat16
I32 = mybir.dt.int32
U32 = mybir.dt.uint32
U16 = mybir.dt.uint16
U8 = mybir.dt.uint8
FP8X4 = mybir.dt.float8_e4m3fn_x4
SIGMOID = mybir.ActivationFunctionType.Sigmoid
MULT = mybir.AluOpType.mult
ADD = mybir.AluOpType.add

P = 128
PACK = 4
GROUP = 16
BLOCK_PARTITIONS = 8
QUADRANT = 32
PLANE_ROWS = QUADRANT // BLOCK_PARTITIONS
HALF = S // 2
LINE = 2
FIRST_WORDS = 512


def tile_picked_ngramgate_none_p_kernel(tc, x_words, x_scales, w1, w2, w3, offs, own, out):
    nc = tc.nc
    with ExitStack() as ctx:
        keep = ctx.enter_context(tc.tile_pool(name="keep", bufs=1))
        psum = ctx.enter_context(tc.psum_pool(name="psum", bufs=1))

        weights = {"w1": w1, "w2": w2, "w3": w3}
        spaces = {}
        raw = {}

        def load_parts(name, first, count, room=0):
            tag = "%s_%d_raw" % (name, first)
            space = keep.tile([P, PACK * (room + count * P)], F32, name=tag, tag=tag, align_bytes=64)
            spaces[name, first] = space
            tile = space[:].rearrange("p (j n) -> p j n", j=PACK)[:, :, room:]
            columns = weights[name][:, first * P : (first + count) * P]
            nc.sync.dma_start(out=tile, in_=columns.rearrange("(p j) n -> p j n", j=PACK))
            for b in range(count):
                raw[name, first + b] = (tile, b * P)

        offs_sb = keep.tile([P, S // GROUP], U16, name="offs_sb")
        own_sb = keep.tile([P, S // GROUP], U16, name="own_sb")
        byte_table = keep.tile([P, T], U8, name="byte_table", align_bytes=64)
        nc.vector.memset(byte_table[:].bitcast(I32), 0)
        x_plane = keep.tile([P, 2 * S], U8, name="x_plane", align_bytes=64)
        nc.vector.memset(x_plane[:].bitcast(I32), 0)
        word_table = keep.tile([P, T], U32, name="word_table", align_bytes=64)

        def load_words(c0, c1):
            source = x_words[0, :, c0:c1, :].rearrange("p c r -> p (c r)").bitcast(I32)
            nc.sync.dma_start(out=word_table[:, c0:c1].bitcast(I32), in_=source)

        load_words(0, FIRST_WORDS)
        nc.sync.dma_start(offs_sb[:], offs)
        nc.sync.dma_start(own_sb[:], own)
        nc.sync.dma_start(out=byte_table[0:P:BLOCK_PARTITIONS, :].bitcast(I32), in_=x_scales[0].bitcast(I32))
        load_parts("w3", 0, 4)
        load_words(FIRST_WORDS, T)
        load_parts("w1", 0, 2)

        warm_in = keep.tile([P, 1], F32, name="warm_in")
        warm_out = keep.tile([P, 1], F32, name="warm_out")
        nc.vector.memset(warm_in[:], 0.0)
        nc.scalar.activation(warm_out[:], warm_in[:], SIGMOID)

        picked_bytes = keep.tile([P, 2 * S], U8, name="picked_bytes", align_bytes=64)
        nc.vector.tensor_copy(picked_bytes[:, 0:S], byte_table[:].indirect(offs_sb[:]))
        nc.vector.tensor_copy(picked_bytes[:, S : 2 * S], byte_table[:].indirect(own_sb[:]))
        for i in range(PLANE_ROWS):
            nc.sync.dma_start(
                out=x_plane[i:P:QUADRANT, :].bitcast(I32),
                in_=picked_bytes[BLOCK_PARTITIONS * i : P : QUADRANT, :].bitcast(I32),
            )

        load_parts("w2", 0, 2)
        load_parts("w1", 2, 2, HALF - P // 2)
        load_parts("w2", 2, 1)
        load_parts("w2", 3, 1)

        on_scalar, on_vector = nc.scalar.copy, nc.vector.tensor_copy
        quantised = {}
        banks = {}
        sums = {}
        gate_ps = {}
        gates = {}

        def grouped_tile(name, first, count):
            label = "%s_%d_grouped" % (name, first)
            return keep.tile([P, count * P, PACK], BF16, name=label, tag=label, align_bytes=64)

        def interleave(copy, grouped, place, name, first, count, skip=0, width=None):
            tile, c0 = raw[name, first]
            width = width or count * P
            source = tile[:, :, c0 + skip : c0 + skip + width]
            target = grouped[:, place * P + skip : place * P + skip + width, :]
            copy(target.rearrange("p (c i) t -> p c t i", i=LINE), source.rearrange("p t (c i) -> p c t i", i=LINE))

        def interleave_on_gpsimd(grouped, place, name, first):
            tile, c0 = raw[name, first]
            source = tile[:, :, c0 : c0 + P].rearrange("p t c -> p c t")
            nc.gpsimd.tensor_scalar(grouped[:, place * P : (place + 1) * P, :], source, 1.0, 0.0, MULT, ADD)

        def quantise(grouped, name, first, parts=None):
            count = grouped.shape[1] // P
            label = "%s_%d" % (name, first)
            words = keep.tile([P, count * P], U32, name=label + "_words", tag=label + "_words", align_bytes=64)
            plane = keep.tile([P, count * P], U8, name=label + "_plane", align_bytes=64)
            nc.vector.quantize_mx(out=words[:].bitcast(FP8X4), scales=plane[:], in_=grouped[:].rearrange("p n t -> p (n t)"))
            for b in range(count):
                quantised[parts[b] if parts else (name, first + b)] = (words[:, b * P : (b + 1) * P], plane[:, b * P : (b + 1) * P])
            return words[:], plane[:]

        def half_columns(half):
            return slice(0, S) if half is None else slice(half * HALF, (half + 1) * HALF)

        def multiply(name, b, half, target, opener="w1"):
            words, plane = quantised[name, b]
            moving_words, moving_plane = x_own if name == "w2" else x_hashed
            columns = half_columns(half)
            nc.tensor.matmul_mx(
                out=target,
                lhsT=words.bitcast(FP8X4),
                lhsT_scale=plane,
                rhs=moving_words[:, columns].bitcast(FP8X4),
                rhs_scale=moving_plane[:, columns],
                start=name in ("w3", opener),
                stop=name != opener,
            )

        def add(name, b):
            for half, target in banks[b]:
                multiply(name, b, half, target)

        def whole_bank(b, tag):
            bank = psum.tile([P, S], F32, name="sum_ps%d" % b, tag=tag)
            banks[b] = [(None, bank[:])]
            for half in (0, 1):
                sums[b, half] = bank[:, half_columns(half)]

        def two_banks(b, tags):
            banks[b] = []
            for half in (0, 1):
                bank = psum.tile([P, S], F32, name="sum_ps%d_%d" % (b, half), tag=tags[half])
                banks[b].append((half, bank[:, 0:HALF]))
                sums[b, half] = bank[:, 0:HALF]

        def gate_pass(b, tag):
            gate_ps[b] = psum.tile([P, S], F32, name="gate_ps%d" % b, tag=tag)
            multiply("w3", b, None, gate_ps[b][:])

        def behind(tag, halves):
            return keep.tile([P, halves, HALF], F32, name="behind_" + tag, tag=tag, align_bytes=64)

        def make_gate(b, tile, place, pieces):
            target = tile[:, place : place + 2, :].rearrange("p h c -> p (h c)")
            for piece in range(pieces):
                columns = slice(piece * S // pieces, (piece + 1) * S // pieces)
                nc.scalar.activation(target[:, columns], gate_ps[b][:, columns], SIGMOID)
            for half in (0, 1):
                gates[b, half] = tile[:, place + half, :]

        def half_gate(b, half, target):
            nc.scalar.activation(target, gate_ps[b][:, half_columns(half)], SIGMOID)
            gates[b, half] = target

        def finish(b, half, result):
            nc.vector.tensor_tensor(result, sums[b, half], gates[b, half], MULT)
            nc.sync.dma_start(out=out[b * P : (b + 1) * P, half_columns(half)], in_=result)

        w3_low, w3_high = grouped_tile("w3", 0, 2), grouped_tile("w3", 2, 2)
        interleave(on_scalar, w3_low, 0, "w3", 0, 1)
        interleave(on_vector, w3_low, 1, "w3", 1, 1)
        interleave(on_vector, w3_high, 0, "w3", 2, 2, 0, 3 * P // 2)
        interleave(on_scalar, w3_high, 0, "w3", 2, 2, 3 * P // 2, P // 2)
        quantise(w3_low, "w3", 0)
        high_words, high_plane = quantise(w3_high, "w3", 2)

        warm_ps = psum.tile([P, S], F32, name="warm_ps", tag="sum2")
        warm_words, warm_plane = quantised["w3", 3]
        for half in (0, 1):
            nc.tensor.matmul_mx(
                out=warm_ps[:, half_columns(half)],
                lhsT=warm_words.bitcast(FP8X4),
                lhsT_scale=warm_plane,
                rhs=high_words.bitcast(FP8X4),
                rhs_scale=high_plane,
                start=True,
                stop=True,
            )

        hashed_words = keep.tile([P, S], U32, name="hashed_words", align_bytes=64)
        own_words = keep.tile([P, S], U32, name="own_words", align_bytes=64)
        nc.vector.tensor_copy(hashed_words[:], word_table[:].indirect(offs_sb[:]))
        nc.vector.tensor_copy(own_words[:], word_table[:].indirect(own_sb[:]))
        x_hashed = (hashed_words[:], x_plane[:, 0:S])
        x_own = (own_words[:], x_plane[:, S : 2 * S])
        first_ps = []
        for half, tag in enumerate(("gate_ps0", "gate_ps0_1")):
            bank = psum.tile([P, S], F32, name="gate_ps0_%d" % half, tag=tag)
            first_ps.append(bank[:, 0:HALF])
            multiply("w3", 0, half, first_ps[half])
        for b in (1, 2):
            gate_pass(b, "gate_ps%d" % b)

        w1_first, second = grouped_tile("w1", 0, 1), grouped_tile("second", 1, 2)
        w1_high = grouped_tile("w1", 2, 2)
        w2_grouped = {b: grouped_tile("w2", b, 1) for b in (0, 2, 3)}
        interleave(on_scalar, w1_first, 0, "w1", 0, 1)
        interleave_on_gpsimd(second, 0, "w1", 1)
        early_gates = behind("w1_0_raw", 5)
        for half in (0, 1):
            nc.scalar.activation(early_gates[:, half, :], first_ps[half], SIGMOID)
            gates[0, half] = early_gates[:, half, :]
        make_gate(1, early_gates, 2, 1)
        half_gate(2, 0, early_gates[:, 4, :])
        quantise(w1_first, "w1", 0)
        interleave(on_vector, w2_grouped[0], 0, "w2", 0, 1)
        interleave(on_vector, second, 1, "w2", 1, 1)
        quantise(w2_grouped[0], "w2", 0)
        quantise(second, "second", 1, (("w1", 1), ("w2", 1)))

        interleave(on_vector, w1_high, 0, "w1", 2, 2, 0, 64)
        interleave(on_vector, w1_high, 0, "w1", 2, 2, 64, 64)
        interleave(on_scalar, w1_high, 0, "w1", 2, 2, 128, 128)
        interleave(on_scalar, w2_grouped[2], 0, "w2", 2, 1)
        interleave(on_scalar, w2_grouped[3], 0, "w2", 3, 1, 0, 96)

        two_banks(0, ("sum0_0", "sum0_1"))
        whole_bank(1, "sum1")
        whole_bank(2, "sum2")
        two_banks(3, ("gate_ps0", "gate_ps1"))
        for (half, target), order in zip(banks[0], (("w1", "w2"), ("w2", "w1"))):
            for name in order:
                multiply(name, 0, half, target, order[0])
        add("w1", 1)
        add("w2", 1)

        pitch = spaces["w1", 2].shape[1] // PACK
        finish(0, 0, spaces["w1", 2][:, 0:HALF])
        gate_pass(3, "sum0_0")
        finish(0, 1, spaces["w1", 2][:, pitch : pitch + HALF])
        quantise(w1_high, "w1", 2)
        add("w1", 2)
        interleave(on_vector, w2_grouped[3], 0, "w2", 3, 1, 96, 32)
        quantise(w2_grouped[2], "w2", 2)
        add("w2", 2)
        add("w1", 3)
        late = behind("w2_2_raw", 4)
        finish(1, 0, late[:, 0, :])
        quantise(w2_grouped[3], "w2", 3)
        add("w2", 3)

        half_gate(2, 1, late[:, 1, :])
        make_gate(3, late, 2, 2)
        finish(1, 1, behind("w2_3_raw", 1)[:, 0, :])
        for b in (2, 3):
            for half in (0, 1):
                result = keep.tile([P, HALF], F32, name="result%d_%d" % (b, half), align_bytes=64)
                finish(b, half, result[:])
